import numpy as np
import ml_dtypes


def mxq(x, axis, fmt="e4m3"):
    dtype, down = {"e4m3": (ml_dtypes.float8_e4m3fn, 7), "e5m2": (ml_dtypes.float8_e5m2, 14)}[fmt]
    v = np.moveaxis(np.asarray(x, np.float32).astype(ml_dtypes.bfloat16).astype(np.float64), axis, -1)
    blocks = v.reshape(v.shape[:-1] + (-1, 32))
    amax = np.abs(blocks).max(-1, keepdims=True)
    byte = np.maximum(np.where(amax > 0, np.frexp(amax)[1] - 1 + 127, 0) - down, 1)
    scale = np.exp2(byte - 127.0)
    codes = (blocks / scale).astype(np.float32).astype(dtype).astype(np.float64)
    return np.moveaxis((codes * scale).reshape(v.shape), -1, axis)


WIDE = False


def mx_kscale(k):
    if not WIDE:
        return np.ones(k)
    levels = np.array([10, -10, 5, -5, 0])
    if k % 512:
        return np.exp2(np.random.permutation(np.resize(levels, k // 32))).repeat(32)
    a = np.empty((k // 512, 16))
    for p in range(k // 512):
        a[p, :8] = np.random.permutation(np.resize(levels, 8))
        for g in range(8):
            far = levels[np.abs(levels - a[p, g]) >= 10]
            a[p, g + 8] = far[np.random.randint(len(far))]
    return np.exp2(a.ravel()).repeat(32)


def f64(x):
    return np.asarray(x).astype(np.float64)


def striped(idx):
    return np.tile(idx.reshape(-1, 16).T, (8, 1)).astype(np.uint16)


def unstriped(offs):
    return offs[:16].T.reshape(-1).astype(np.int64)


def striped8(idx):
    return np.concatenate([x.reshape(-1, 16).T for x in idx]).astype(np.uint16)


def runs(offs, k):
    lists = np.stack([offs[16 * r : 16 * r + 16].T.reshape(-1) for r in range(8)]).astype(np.int64)
    return lists[np.arange(k) % 512 // 64]


def pack_weight(w):
    k, n = w.shape
    w = f64(np.asarray(w, np.float32).astype(ml_dtypes.bfloat16)).reshape(k // 32, 32, n)
    amax = np.abs(w).max(1)
    byte = np.clip(np.where(amax > 0, np.frexp(amax)[1] - 1 + 127 - 7, 1), 1, 254)
    scaled = (w * np.exp2(127.0 - byte)[:, None, :]).reshape(k, n).astype(np.float32)
    words = np.ascontiguousarray(scaled.reshape(k // 512, 128, 4, n).transpose(0, 1, 3, 2)).astype(ml_dtypes.float8_e4m3fn).view(np.uint8)
    return words, np.ascontiguousarray(byte.astype(np.uint8).reshape(k // 512, 16, n))


def unpack_weight(words, scales):
    g, p, n, _ = words.shape
    vals = np.ascontiguousarray(words).view(ml_dtypes.float8_e4m3fn).astype(np.float64) * np.repeat(np.exp2(scales.astype(np.float64) - 127.0), 8, axis=1)[..., None]
    return vals.transpose(0, 1, 3, 2).reshape(g * 512, n)


def relu(v):
    return np.maximum(v, 0.0)


K, T, S, N, G, H = 512, 2048, 512, 512, 2048, 512


def setup_inputs():
    n = np.random.standard_normal
    s = mx_kscale(K)[:, None]
    u = mx_kscale(H)
    packed_xT = pack_weight(n((K, T)) * s)
    packed_dT = pack_weight(n((K, G)) / s)
    return {
        "x_words": packed_xT[0],
        "x_scales": packed_xT[1],
        "d_words": packed_dT[0],
        "d_scales": packed_dT[1],
        "gn": (np.random.uniform(0.5, 1.5, (H, 1)) * u[:, None]).astype(np.float32),
        "w1": (n((H, N)) / np.sqrt(H) / u[:, None]).astype(np.float32),
        "offs": striped(np.random.permutation(T)[:S]),
        "kidx": striped8(np.random.randint(0, G, (8, H))),
        "nb": striped8(np.stack([np.random.permutation(S) for _ in range(8)])),
    }


def reference(x_words, x_scales, d_words, d_scales, gn, w1, offs, kidx, nb):
    d_kidx = unpack_weight(d_words, d_scales)[np.arange(K)[:, None], runs(kidx, K)]
    xq = unpack_weight(x_words, x_scales)[:, unstriped(offs)]
    s = 0.0625 * (d_kidx.T @ xq)
    z = f64(gn) * (relu(s + 0.5 * (s[np.arange(H)[:, None], runs(nb, H)])))
    return mxq(f64(w1), 0, "e4m3").T @ mxq(z, 0, "e4m3")

@@ -1,0 +1,194 @@
+from contextlib import ExitStack
+
+import concourse.mybir as mybir
+
+K, T, S, N, G, H = 512, 2048, 512, 512, 2048, 512
+FLOPS = 2 * K * H * S + 2 * H * N * S
+
+F32 = mybir.dt.float32
+BF16 = mybir.dt.bfloat16
+I32 = mybir.dt.int32
+U32 = mybir.dt.uint32
+U16 = mybir.dt.uint16
+U8 = mybir.dt.uint8
+FP8X4 = mybir.dt.float8_e4m3fn_x4
+ACT = mybir.ActivationFunctionType
+ALU = mybir.AluOpType
+
+P = 128
+PACK = 4
+HALF = 256
+PIECES = (256, 128, 128)
+
+
+def tile_picked_scoremix_relu_p_kernel(tc, x_words, x_scales, d_words, d_scales, gn, w1, offs, kidx, nb, out):
+    nc = tc.nc
+    with ExitStack() as ctx:
+        keep = ctx.enter_context(tc.tile_pool(name="keep", bufs=1))
+        psum = ctx.enter_context(tc.psum_pool(name="psum", bufs=8))
+
+        kidx_sb = keep.tile([P, H // 16], U16, name="kidx_sb")
+        offs_sb = keep.tile([P, S // 16], U16, name="offs_sb")
+        nb_sb = keep.tile([P, S // 16], U16, name="nb_sb")
+        nc.sync.dma_start(kidx_sb[:], kidx)
+        nc.sync.dma_start(offs_sb[:], offs)
+        nc.sync.dma_start(nb_sb[:], nb)
+
+        gn_sb = keep.tile([P, PACK], F32, name="gn_sb")
+        nc.gpsimd.dma_start(gn_sb[:], gn.rearrange("(p t) o -> p (t o)", t=PACK))
+
+        w_rows = w1.rearrange("(p t) m -> p t m", t=PACK)
+        w_raw = []
+        for a in range(2):
+            raw = keep.tile([P, PACK, HALF], F32, name="w_raw%d" % a)
+            nc.sync.dma_start(raw[:], w_rows[:, :, a * HALF : (a + 1) * HALF])
+            w_raw.append(raw)
+
+        dw_win = keep.tile([P, G], I32, name="dw_win")
+        xw_win = keep.tile([P, T], I32, name="xw_win")
+        nc.sync.dma_start(dw_win[:], d_words[0].rearrange("p n t -> p (n t)").bitcast(I32))
+        nc.sync.dma_start(xw_win[:], x_words[0].rearrange("p n t -> p (n t)").bitcast(I32))
+
+        ds_win = keep.tile([P, G], U8, name="ds_win")
+        xs_win = keep.tile([P, T], U8, name="xs_win", tag="x_turn", align_bytes=64)
+        nc.vector.memset(ds_win[:].bitcast(I32), 0)
+        nc.vector.memset(xs_win[:].bitcast(I32), 0)
+        ds_rows = d_scales[0].bitcast(I32)
+        xs_rows = x_scales[0].bitcast(I32)
+        for e in range(2):
+            nc.scalar.dma_start(ds_win[e:P:16, :].bitcast(I32), ds_rows[e:16:2, :])
+        for b in range(4):
+            queue = nc.scalar if b < 2 else nc.gpsimd
+            queue.dma_start(xs_win[b:P:32, :].bitcast(I32), xs_rows[b:16:4, :])
+
+        ds_got = keep.tile([P, H], U8, name="ds_got")
+        nc.vector.tensor_copy(ds_got[:], ds_win[:].indirect(kidx_sb[:]))
+        ds_dealt = keep.tile([P, H], U8, name="ds_dealt")
+        nc.vector.tensor_copy(
+            ds_dealt[:].rearrange("p (t m) -> p t m", t=PACK), ds_got[:].rearrange("p (m t) -> p t m", t=PACK)
+        )
+        d_scale = keep.tile([P, H], U8, name="d_scale", align_bytes=64)
+        nc.vector.tensor_copy(d_scale[:].bitcast(I32), ds_dealt[:].bitcast(I32))
+        for e in range(2):
+            nc.sync.dma_start(d_scale[2 + e : P : 32, :].bitcast(I32), ds_dealt[16 + e : P : 32, :].bitcast(I32))
+
+        xs_got = keep.tile([P, S], U8, name="xs_got", align_bytes=64)
+        nc.vector.tensor_copy(xs_got[:], xs_win[:].indirect(offs_sb[:]))
+
+        gn_sign = keep.tile([P, PACK], F32, name="gn_sign")
+        gn_half = keep.tile([P, PACK], F32, name="gn_half")
+        nc.scalar.activation(gn_sign[:], gn_sb[:], ACT.Sign)
+        nc.scalar.activation(gn_half[:], gn_sb[:], ACT.Abs, scale=0.0625 * 0.5)
+
+        w_codes = keep.tile([P, N], U32, name="w_codes", align_bytes=64)
+        w_scales = keep.tile([P, N], U8, name="w_scales", align_bytes=64)
+        w_grouped = []
+        for a in range(2):
+            signed = keep.tile([P, PACK, HALF], BF16, name="w_signed%d" % a)
+            for t in range(PACK):
+                nc.scalar.activation(signed[:, t, :], w_raw[a][:, t, :], ACT.Copy, scale=gn_sign[:, t : t + 1])
+            grouped = keep.tile([P, HALF, PACK], BF16, name="w_grouped%d" % a, align_bytes=64)
+            nc.scalar.copy(
+                grouped[:].rearrange("p (c i) t -> p c t i", i=4),
+                signed[:].rearrange("p t (c i) -> p c t i", i=4),
+            )
+            w_grouped.append(grouped)
+
+        def quantize_w(a):
+            cols = slice(a * HALF, (a + 1) * HALF)
+            nc.vector.quantize_mx(
+                out=w_codes[:, cols].bitcast(FP8X4),
+                scales=w_scales[:, cols],
+                in_=w_grouped[a][:].rearrange("p m t -> p (m t)"),
+            )
+
+        quantize_w(0)
+        dw_got = keep.tile([P, H], U32, name="dw_got")
+        nc.vector.tensor_copy(dw_got[:], dw_win[:].bitcast(U32).indirect(kidx_sb[:]))
+        d_codes = keep.tile([P, PACK, P], U32, name="d_codes", align_bytes=64)
+        nc.vector.tensor_copy(d_codes[:], dw_got[:].rearrange("p (m t) -> p t m", t=PACK))
+
+        x_codes = []
+        for h in range(2):
+            got = keep.tile([P, HALF], U32, name="x_codes%d" % h, tag="x_turn" if h == 0 else "x_codes", align_bytes=64)
+            nc.vector.tensor_copy(got[:], xw_win[:].bitcast(U32).indirect(offs_sb[:, h * 16 : (h + 1) * 16]))
+            x_codes.append(got)
+        quantize_w(1)
+
+        halved = []
+        for t in range(PACK):
+            row = keep.tile([P, S], F32, name="halved%d" % t)
+            for h in range(2):
+                cols = slice(h * HALF, (h + 1) * HALF)
+                acc = psum.tile([P, HALF], F32, name="acc", tag="bank")
+                nc.tensor.matmul_mx(
+                    out=acc[:],
+                    lhsT=d_codes[:, t, :].bitcast(FP8X4),
+                    lhsT_scale=d_scale[:, t * P : (t + 1) * P],
+                    rhs=x_codes[h][:].bitcast(FP8X4),
+                    rhs_scale=xs_got[:, cols],
+                    start=True,
+                    stop=True,
+                )
+                nc.scalar.activation(row[:, cols], acc[:], ACT.Copy, scale=gn_half[:, t : t + 1])
+            halved.append(row)
+
+        out_rows = out.rearrange("(a p) j -> p a j", p=P)
+
+        def mix(piece, j0, n):
+            mixed = keep.tile([P, PACK, n], F32, name="mixed%d" % j0)
+            got = keep.tile([P, PACK, n], F32, name="got%d" % j0, tag="turn%d" % piece, align_bytes=64)
+
+            def add(t):
+                nc.vector.scalar_tensor_tensor(
+                    mixed[:, t, :], halved[t][:, j0 : j0 + n], 2.0, got[:, t, :], ALU.mult, ALU.add
+                )
+
+            for t in range(PACK):
+                nc.vector.tensor_copy(got[:, t, :], halved[t][:].indirect(nb_sb[:, j0 // 16 : (j0 + n) // 16]))
+                if t > 0:
+                    add(t - 1)
+            add(PACK - 1)
+            z = keep.tile([P, n, PACK], BF16, name="z%d" % j0, tag="turn%d" % (piece + 2), align_bytes=64)
+            nc.scalar.activation(
+                z[:].rearrange("p (c i) t -> p c t i", i=4),
+                mixed[:].rearrange("p t (c i) -> p c t i", i=4),
+                ACT.Relu,
+            )
+            return z
+
+        def project(j0, n, z, last):
+            z_codes = keep.tile([P, n], U32, name="z_codes%d" % j0, align_bytes=64)
+            z_scales = keep.tile([P, n], U8, name="z_scales%d" % j0, align_bytes=64)
+            nc.vector.quantize_mx(
+                out=z_codes[:].bitcast(FP8X4), scales=z_scales[:], in_=z[:].rearrange("p j t -> p (j t)")
+            )
+            for pair in range(2):
+                acc = psum.tile([P, 2, n], F32, name="acc2", tag="bank")
+                for a in range(2):
+                    m_cols = slice((2 * pair + a) * P, (2 * pair + a + 1) * P)
+                    nc.tensor.matmul_mx(
+                        out=acc[:, a, :],
+                        lhsT=w_codes[:, m_cols].bitcast(FP8X4),
+                        lhsT_scale=w_scales[:, m_cols],
+                        rhs=z_codes[:].bitcast(FP8X4),
+                        rhs_scale=z_scales[:],
+                        start=True,
+                        stop=True,
+                    )
+                res = keep.tile([P, 2, n], F32, name="res%d_%d" % (j0, pair))
+                if last and pair == 1:
+                    nc.vector.tensor_copy(res[:], acc[:])
+                else:
+                    nc.scalar.copy(res[:], acc[:])
+                nc.sync.dma_start(out_rows[:, 2 * pair : 2 * pair + 2, j0 : j0 + n], res[:])
+
+        waiting = None
+        j0 = 0
+        for piece, n in enumerate(PIECES):
+            z = mix(piece, j0, n)
+            if waiting is not None:
+                project(*waiting, False)
+            waiting = (j0, n, z)
+            j0 = j0 + n
+        project(*waiting, True)

@@ -18,7 +18,7 @@ ALU = mybir.AluOpType
 P = 128
 PACK = 4
 HALF = 256
-PIECES = (256, 128, 128)
+PIECE = 128
 
 
 def tile_picked_scoremix_relu_p_kernel(tc, x_words, x_scales, d_words, d_scales, gn, w1, offs, kidx, nb, out):
@@ -30,12 +30,19 @@ def tile_picked_scoremix_relu_p_kernel(tc, x_words, x_scales, d_words, d_scales,
         kidx_sb = keep.tile([P, H // 16], U16, name="kidx_sb")
         offs_sb = keep.tile([P, S // 16], U16, name="offs_sb")
         nb_sb = keep.tile([P, S // 16], U16, name="nb_sb")
-        nc.sync.dma_start(kidx_sb[:], kidx)
-        nc.sync.dma_start(offs_sb[:], offs)
-        nc.sync.dma_start(nb_sb[:], nb)
-
         gn_sb = keep.tile([P, PACK], F32, name="gn_sb")
-        nc.gpsimd.dma_start(gn_sb[:], gn.rearrange("(p t) o -> p (t o)", t=PACK))
+        nc.sync.dma_start(kidx_sb[:], kidx)
+        nc.scalar.dma_start(gn_sb[:], gn.rearrange("(p t) o -> p (t o)", t=PACK))
+        nc.sync.dma_start(offs_sb[:], offs)
+
+        ds_win = keep.tile([P, G], U8, name="ds_win")
+        xs_win = keep.tile([P, T], U8, name="xs_win")
+        nc.vector.memset(ds_win[:].bitcast(I32), 0)
+        nc.vector.memset(xs_win[:].bitcast(I32), 0)
+        for e in range(2):
+            nc.sync.dma_start(ds_win[e:P:16, :].bitcast(I32), d_scales[0].bitcast(I32)[e:16:2, :])
+        for e in range(2):
+            nc.scalar.dma_start(xs_win[e:P:16, :].bitcast(I32), x_scales[0].bitcast(I32)[e:16:2, :])
 
         w_rows = w1.rearrange("(p t) m -> p t m", t=PACK)
         w_raw = []
@@ -43,130 +50,90 @@ def tile_picked_scoremix_relu_p_kernel(tc, x_words, x_scales, d_words, d_scales,
             raw = keep.tile([P, PACK, HALF], F32, name="w_raw%d" % a)
             nc.sync.dma_start(raw[:], w_rows[:, :, a * HALF : (a + 1) * HALF])
             w_raw.append(raw)
-
         dw_win = keep.tile([P, G], I32, name="dw_win")
-        xw_win = keep.tile([P, T], I32, name="xw_win")
         nc.sync.dma_start(dw_win[:], d_words[0].rearrange("p n t -> p (n t)").bitcast(I32))
+        xw_win = keep.tile([P, T], I32, name="xw_win", tag="x_turn", align_bytes=64)
         nc.sync.dma_start(xw_win[:], x_words[0].rearrange("p n t -> p (n t)").bitcast(I32))
-
-        ds_win = keep.tile([P, G], U8, name="ds_win")
-        xs_win = keep.tile([P, T], U8, name="xs_win", tag="x_turn", align_bytes=64)
-        nc.vector.memset(ds_win[:].bitcast(I32), 0)
-        nc.vector.memset(xs_win[:].bitcast(I32), 0)
-        ds_rows = d_scales[0].bitcast(I32)
-        xs_rows = x_scales[0].bitcast(I32)
-        for e in range(2):
-            nc.scalar.dma_start(ds_win[e:P:16, :].bitcast(I32), ds_rows[e:16:2, :])
-        for b in range(4):
-            queue = nc.scalar if b < 2 else nc.gpsimd
-            queue.dma_start(xs_win[b:P:32, :].bitcast(I32), xs_rows[b:16:4, :])
-
-        ds_got = keep.tile([P, H], U8, name="ds_got")
-        nc.vector.tensor_copy(ds_got[:], ds_win[:].indirect(kidx_sb[:]))
-        ds_dealt = keep.tile([P, H], U8, name="ds_dealt")
-        nc.vector.tensor_copy(
-            ds_dealt[:].rearrange("p (t m) -> p t m", t=PACK), ds_got[:].rearrange("p (m t) -> p t m", t=PACK)
-        )
-        d_scale = keep.tile([P, H], U8, name="d_scale", align_bytes=64)
-        nc.vector.tensor_copy(d_scale[:].bitcast(I32), ds_dealt[:].bitcast(I32))
-        for e in range(2):
-            nc.sync.dma_start(d_scale[2 + e : P : 32, :].bitcast(I32), ds_dealt[16 + e : P : 32, :].bitcast(I32))
-
-        xs_got = keep.tile([P, S], U8, name="xs_got", align_bytes=64)
-        nc.vector.tensor_copy(xs_got[:], xs_win[:].indirect(offs_sb[:]))
+        nc.sync.dma_start(nb_sb[:], nb)
 
         gn_sign = keep.tile([P, PACK], F32, name="gn_sign")
         gn_half = keep.tile([P, PACK], F32, name="gn_half")
+        gn_whole = keep.tile([P, PACK], F32, name="gn_whole")
         nc.scalar.activation(gn_sign[:], gn_sb[:], ACT.Sign)
         nc.scalar.activation(gn_half[:], gn_sb[:], ACT.Abs, scale=0.0625 * 0.5)
+        nc.scalar.activation(gn_whole[:], gn_sb[:], ACT.Abs, scale=0.0625)
 
-        w_codes = keep.tile([P, N], U32, name="w_codes", align_bytes=64)
-        w_scales = keep.tile([P, N], U8, name="w_scales", align_bytes=64)
-        w_grouped = []
+        ds_got = keep.tile([P, H], U8, name="ds_got")
+        nc.vector.tensor_copy(ds_got[:], ds_win[:].indirect(kidx_sb[:]))
+
+        both = keep.tile([P, H + S], U8, name="both")
+        nc.vector.tensor_copy(
+            both[:, 0:H].rearrange("p (t m) -> p t m", t=PACK), ds_got[:].rearrange("p (m t) -> p t m", t=PACK)
+        )
+        xs_got = keep.tile([P, S], U8, name="xs_got")
+        nc.vector.tensor_copy(xs_got[:], xs_win[:].indirect(offs_sb[:]))
+        nc.vector.tensor_copy(both[:, H : H + S].bitcast(I32), xs_got[:].bitcast(I32))
+        placed = keep.tile([P, H + S], U8, name="placed", align_bytes=64)
+        nc.vector.tensor_copy(placed[:].bitcast(I32), both[:].bitcast(I32))
+        for e in range(2):
+            nc.sync.dma_start(placed[2 + e : P : 32, :].bitcast(I32), both[16 + e : P : 32, :].bitcast(I32))
+
+        w_grouped = keep.tile([P, N, PACK], BF16, name="w_grouped", align_bytes=64)
         for a in range(2):
             signed = keep.tile([P, PACK, HALF], BF16, name="w_signed%d" % a)
             for t in range(PACK):
                 nc.scalar.activation(signed[:, t, :], w_raw[a][:, t, :], ACT.Copy, scale=gn_sign[:, t : t + 1])
-            grouped = keep.tile([P, HALF, PACK], BF16, name="w_grouped%d" % a, align_bytes=64)
             nc.scalar.copy(
-                grouped[:].rearrange("p (c i) t -> p c t i", i=4),
+                w_grouped[:, a * HALF : (a + 1) * HALF, :].rearrange("p (c i) t -> p c t i", i=4),
                 signed[:].rearrange("p t (c i) -> p c t i", i=4),
             )
-            w_grouped.append(grouped)
 
-        def quantize_w(a):
-            cols = slice(a * HALF, (a + 1) * HALF)
-            nc.vector.quantize_mx(
-                out=w_codes[:, cols].bitcast(FP8X4),
-                scales=w_scales[:, cols],
-                in_=w_grouped[a][:].rearrange("p m t -> p (m t)"),
-            )
-
-        quantize_w(0)
         dw_got = keep.tile([P, H], U32, name="dw_got")
         nc.vector.tensor_copy(dw_got[:], dw_win[:].bitcast(U32).indirect(kidx_sb[:]))
         d_codes = keep.tile([P, PACK, P], U32, name="d_codes", align_bytes=64)
         nc.vector.tensor_copy(d_codes[:], dw_got[:].rearrange("p (m t) -> p t m", t=PACK))
 
-        x_codes = []
+        x_codes = keep.tile([P, S], U32, name="x_codes", align_bytes=64)
         for h in range(2):
-            got = keep.tile([P, HALF], U32, name="x_codes%d" % h, tag="x_turn" if h == 0 else "x_codes", align_bytes=64)
-            nc.vector.tensor_copy(got[:], xw_win[:].bitcast(U32).indirect(offs_sb[:, h * 16 : (h + 1) * 16]))
-            x_codes.append(got)
-        quantize_w(1)
+            nc.vector.tensor_copy(
+                x_codes[:, h * HALF : (h + 1) * HALF],
+                xw_win[:].bitcast(U32).indirect(offs_sb[:, h * 16 : (h + 1) * 16]),
+            )
 
-        halved = []
-        for t in range(PACK):
-            row = keep.tile([P, S], F32, name="halved%d" % t)
-            for h in range(2):
-                cols = slice(h * HALF, (h + 1) * HALF)
-                acc = psum.tile([P, HALF], F32, name="acc", tag="bank")
-                nc.tensor.matmul_mx(
-                    out=acc[:],
-                    lhsT=d_codes[:, t, :].bitcast(FP8X4),
-                    lhsT_scale=d_scale[:, t * P : (t + 1) * P],
-                    rhs=x_codes[h][:].bitcast(FP8X4),
-                    rhs_scale=xs_got[:, cols],
-                    start=True,
-                    stop=True,
-                )
-                nc.scalar.activation(row[:, cols], acc[:], ACT.Copy, scale=gn_half[:, t : t + 1])
-            halved.append(row)
+        w_codes = keep.tile([P, N], U32, name="w_codes", tag="x_turn", align_bytes=64)
+        w_scales = keep.tile([P, N], U8, name="w_scales", align_bytes=64)
+        nc.vector.quantize_mx(
+            out=w_codes[:].bitcast(FP8X4), scales=w_scales[:], in_=w_grouped[:].rearrange("p m t -> p (m t)")
+        )
 
         out_rows = out.rearrange("(a p) j -> p a j", p=P)
 
-        def mix(piece, j0, n):
-            mixed = keep.tile([P, PACK, n], F32, name="mixed%d" % j0)
-            got = keep.tile([P, PACK, n], F32, name="got%d" % j0, tag="turn%d" % piece, align_bytes=64)
-
-            def add(t):
-                nc.vector.scalar_tensor_tensor(
-                    mixed[:, t, :], halved[t][:, j0 : j0 + n], 2.0, got[:, t, :], ALU.mult, ALU.add
-                )
-
-            for t in range(PACK):
-                nc.vector.tensor_copy(got[:, t, :], halved[t][:].indirect(nb_sb[:, j0 // 16 : (j0 + n) // 16]))
-                if t > 0:
-                    add(t - 1)
-            add(PACK - 1)
-            z = keep.tile([P, n, PACK], BF16, name="z%d" % j0, tag="turn%d" % (piece + 2), align_bytes=64)
-            nc.scalar.activation(
-                z[:].rearrange("p (c i) t -> p c t i", i=4),
-                mixed[:].rearrange("p t (c i) -> p c t i", i=4),
-                ACT.Relu,
+        def mix(mixed, t, whole, j0, n):
+            nc.vector.tensor_tensor(
+                mixed[:, t, :], halved[t][:].indirect(nb_sb[:, j0 // 16 : (j0 + n) // 16]), whole, ALU.add
             )
+
+        def rectify(mixed, n, engine, tag):
+            z = keep.tile([P, n, PACK], BF16, name="z_" + tag, tag=tag, align_bytes=64)
+            dst = z[:].rearrange("p (c i) t -> p c t i", i=4)
+            src = mixed[:].rearrange("p t (c i) -> p c t i", i=4)
+            if engine is nc.scalar:
+                nc.scalar.activation(dst, src, ACT.Relu)
+            else:
+                nc.vector.tensor_scalar(dst, src, 0.0, None, ALU.max)
             return z
 
-        def project(j0, n, z, last):
+        def project(z, j0, n, readers):
             z_codes = keep.tile([P, n], U32, name="z_codes%d" % j0, align_bytes=64)
             z_scales = keep.tile([P, n], U8, name="z_scales%d" % j0, align_bytes=64)
             nc.vector.quantize_mx(
                 out=z_codes[:].bitcast(FP8X4), scales=z_scales[:], in_=z[:].rearrange("p j t -> p (j t)")
             )
-            for pair in range(2):
-                acc = psum.tile([P, 2, n], F32, name="acc2", tag="bank")
-                for a in range(2):
-                    m_cols = slice((2 * pair + a) * P, (2 * pair + a + 1) * P)
+            blocks = 4 // len(readers)
+            for r, engine in enumerate(readers):
+                acc = psum.tile([P, blocks, n], F32, name="acc2", tag="bank")
+                for a in range(blocks):
+                    m_cols = slice((r * blocks + a) * P, (r * blocks + a + 1) * P)
                     nc.tensor.matmul_mx(
                         out=acc[:, a, :],
                         lhsT=w_codes[:, m_cols].bitcast(FP8X4),
@@ -176,19 +143,49 @@ def tile_picked_scoremix_relu_p_kernel(tc, x_words, x_scales, d_words, d_scales,
                         start=True,
                         stop=True,
                     )
-                res = keep.tile([P, 2, n], F32, name="res%d_%d" % (j0, pair))
-                if last and pair == 1:
-                    nc.vector.tensor_copy(res[:], acc[:])
-                else:
+                res = keep.tile([P, blocks, n], F32, name="res%d_%d" % (j0, r))
+                if engine is nc.scalar:
                     nc.scalar.copy(res[:], acc[:])
-                nc.sync.dma_start(out_rows[:, 2 * pair : 2 * pair + 2, j0 : j0 + n], res[:])
+                else:
+                    nc.vector.tensor_copy(res[:], acc[:])
+                nc.sync.dma_start(out_rows[:, r * blocks : (r + 1) * blocks, j0 : j0 + n], res[:])
 
-        waiting = None
-        j0 = 0
-        for piece, n in enumerate(PIECES):
-            z = mix(piece, j0, n)
-            if waiting is not None:
-                project(*waiting, False)
-            waiting = (j0, n, z)
-            j0 = j0 + n
-        project(*waiting, True)
+        halved = []
+        right = []
+        mixed_a = keep.tile([P, PACK, HALF], F32, name="mixed_a")
+        for t in range(PACK):
+            row = keep.tile([P, S], F32, name="halved%d" % t)
+            left = keep.tile([P, HALF], F32, name="left%d" % t, tag="left%d" % t)
+            for h in range(2):
+                cols = slice(h * HALF, (h + 1) * HALF)
+                acc = psum.tile([P, HALF], F32, name="acc", tag="bank")
+                nc.tensor.matmul_mx(
+                    out=acc[:],
+                    lhsT=d_codes[:, t, :].bitcast(FP8X4),
+                    lhsT_scale=placed[:, t * P : (t + 1) * P],
+                    rhs=x_codes[:, cols].bitcast(FP8X4),
+                    rhs_scale=placed[:, H + h * HALF : H + (h + 1) * HALF],
+                    start=True,
+                    stop=True,
+                )
+                nc.scalar.activation(row[:, cols], acc[:], ACT.Copy, scale=gn_half[:, t : t + 1])
+                if h == 0:
+                    nc.scalar.activation(left[:], acc[:], ACT.Copy, scale=gn_whole[:, t : t + 1])
+            halved.append(row)
+            mix(mixed_a, t, left[:], 0, HALF)
+            doubled = keep.tile([P, HALF], F32, name="right%d" % t)
+            nc.vector.tensor_scalar(doubled[:], row[:, HALF:S], 2.0, None, ALU.mult)
+            right.append(doubled)
+
+        z_a = rectify(mixed_a, HALF, nc.scalar, "a")
+        mixed_b = keep.tile([P, PACK, PIECE], F32, name="mixed_b", tag="left3")
+        for t in range(PACK):
+            mix(mixed_b, t, right[t][:, 0:PIECE], HALF, PIECE)
+        z_b = rectify(mixed_b, PIECE, nc.scalar, "b")
+        project(z_a, 0, HALF, (nc.scalar, nc.scalar))
+        mixed_c = keep.tile([P, PACK, PIECE], F32, name="mixed_c", tag="a", align_bytes=64)
+        for t in range(PACK):
+            mix(mixed_c, t, right[t][:, PIECE:HALF], HALF + PIECE, PIECE)
+        project(z_b, HALF, PIECE, (nc.scalar,))
+        z_c = rectify(mixed_c, PIECE, nc.vector, "c")
+        project(z_c, HALF + PIECE, PIECE, (nc.scalar, nc.vector))

@@ -32,8 +32,12 @@ def tile_picked_scoremix_relu_p_kernel(tc, x_words, x_scales, d_words, d_scales,
         nb_sb = keep.tile([P, S // 16], U16, name="nb_sb")
         gn_sb = keep.tile([P, PACK], F32, name="gn_sb")
         nc.sync.dma_start(kidx_sb[:], kidx)
+        w_rows = w1.rearrange("(p t) m -> p t m", t=PACK)
+        w_raw = [keep.tile([P, PACK, HALF], F32, name="w_raw%d" % a) for a in range(2)]
+        nc.scalar.dma_start(w_raw[0][:], w_rows[:, :, 0:HALF])
         nc.scalar.dma_start(gn_sb[:], gn.rearrange("(p t) o -> p (t o)", t=PACK))
         nc.sync.dma_start(offs_sb[:], offs)
+        nc.sync.dma_start(nb_sb[:], nb)
 
         ds_win = keep.tile([P, G], U8, name="ds_win")
         xs_win = keep.tile([P, T], U8, name="xs_win")
@@ -44,17 +48,11 @@ def tile_picked_scoremix_relu_p_kernel(tc, x_words, x_scales, d_words, d_scales,
         for e in range(2):
             nc.scalar.dma_start(xs_win[e:P:16, :].bitcast(I32), x_scales[0].bitcast(I32)[e:16:2, :])
 
-        w_rows = w1.rearrange("(p t) m -> p t m", t=PACK)
-        w_raw = []
-        for a in range(2):
-            raw = keep.tile([P, PACK, HALF], F32, name="w_raw%d" % a)
-            nc.sync.dma_start(raw[:], w_rows[:, :, a * HALF : (a + 1) * HALF])
-            w_raw.append(raw)
+        nc.sync.dma_start(w_raw[1][:], w_rows[:, :, HALF:N])
         dw_win = keep.tile([P, G], I32, name="dw_win")
         nc.sync.dma_start(dw_win[:], d_words[0].rearrange("p n t -> p (n t)").bitcast(I32))
         xw_win = keep.tile([P, T], I32, name="xw_win", tag="x_turn", align_bytes=64)
         nc.sync.dma_start(xw_win[:], x_words[0].rearrange("p n t -> p (n t)").bitcast(I32))
-        nc.sync.dma_start(nb_sb[:], nb)
 
         gn_sign = keep.tile([P, PACK], F32, name="gn_sign")
         gn_half = keep.tile([P, PACK], F32, name="gn_half")
@@ -68,7 +66,8 @@ def tile_picked_scoremix_relu_p_kernel(tc, x_words, x_scales, d_words, d_scales,
 
         both = keep.tile([P, H + S], U8, name="both")
         nc.vector.tensor_copy(
-            both[:, 0:H].rearrange("p (t m) -> p t m", t=PACK), ds_got[:].rearrange("p (m t) -> p t m", t=PACK)
+            both[:, 0:H].rearrange("p (t c i) -> p c t i", t=PACK, i=16),
+            ds_got[:].rearrange("p (c i t) -> p c t i", t=PACK, i=16),
         )
         xs_got = keep.tile([P, S], U8, name="xs_got")
         nc.vector.tensor_copy(xs_got[:], xs_win[:].indirect(offs_sb[:]))
@@ -91,7 +90,9 @@ def tile_picked_scoremix_relu_p_kernel(tc, x_words, x_scales, d_words, d_scales,
         dw_got = keep.tile([P, H], U32, name="dw_got")
         nc.vector.tensor_copy(dw_got[:], dw_win[:].bitcast(U32).indirect(kidx_sb[:]))
         d_codes = keep.tile([P, PACK, P], U32, name="d_codes", align_bytes=64)
-        nc.vector.tensor_copy(d_codes[:], dw_got[:].rearrange("p (m t) -> p t m", t=PACK))
+        nc.vector.tensor_copy(
+            d_codes[:].rearrange("p t (c i) -> p c t i", i=4), dw_got[:].rearrange("p (c i t) -> p c t i", t=PACK, i=4)
+        )
 
         x_codes = keep.tile([P, S], U32, name="x_codes", align_bytes=64)
         for h in range(2):
@@ -174,7 +175,10 @@ def tile_picked_scoremix_relu_p_kernel(tc, x_words, x_scales, d_words, d_scales,
             halved.append(row)
             mix(mixed_a, t, left[:], 0, HALF)
             doubled = keep.tile([P, HALF], F32, name="right%d" % t)
-            nc.vector.tensor_scalar(doubled[:], row[:, HALF:S], 2.0, None, ALU.mult)
+            if t < PACK - 1:
+                nc.vector.tensor_scalar(doubled[:], row[:, HALF:S], 2.0, None, ALU.mult)
+            else:
+                nc.scalar.activation(doubled[:], acc[:], ACT.Copy, scale=gn_whole[:, t : t + 1])
             right.append(doubled)
 
         z_a = rectify(mixed_a, HALF, nc.scalar, "a")

@@ -33,8 +33,8 @@ def tile_picked_scoremix_relu_p_kernel(tc, x_words, x_scales, d_words, d_scales,
         gn_sb = keep.tile([P, PACK], F32, name="gn_sb")
         nc.sync.dma_start(kidx_sb[:], kidx)
         w_rows = w1.rearrange("(p t) m -> p t m", t=PACK)
-        w_raw = [keep.tile([P, PACK, HALF], F32, name="w_raw%d" % a) for a in range(2)]
-        nc.scalar.dma_start(w_raw[0][:], w_rows[:, :, 0:HALF])
+        w_early = keep.tile([P, PACK, HALF], F32, name="w_early")
+        nc.scalar.dma_start(w_early[:], w_rows[:, :, 0:HALF])
         nc.scalar.dma_start(gn_sb[:], gn.rearrange("(p t) o -> p (t o)", t=PACK))
         nc.sync.dma_start(offs_sb[:], offs)
         nc.sync.dma_start(nb_sb[:], nb)
@@ -42,15 +42,14 @@ def tile_picked_scoremix_relu_p_kernel(tc, x_words, x_scales, d_words, d_scales,
         ds_win = keep.tile([P, G], U8, name="ds_win")
         xs_win = keep.tile([P, T], U8, name="xs_win")
         nc.vector.memset(ds_win[:].bitcast(I32), 0)
-        nc.vector.memset(xs_win[:].bitcast(I32), 0)
-        for e in range(2):
-            nc.sync.dma_start(ds_win[e:P:16, :].bitcast(I32), d_scales[0].bitcast(I32)[e:16:2, :])
-        for e in range(2):
-            nc.scalar.dma_start(xs_win[e:P:16, :].bitcast(I32), x_scales[0].bitcast(I32)[e:16:2, :])
+        nc.gpsimd.memset(xs_win[:].bitcast(I32), 0)
+        nc.sync.dma_start(ds_win[0:P:8, :].bitcast(I32), d_scales[0].bitcast(I32))
+        nc.sync.dma_start(xs_win[0:P:8, :].bitcast(I32), x_scales[0].bitcast(I32))
 
-        nc.sync.dma_start(w_raw[1][:], w_rows[:, :, HALF:N])
         dw_win = keep.tile([P, G], I32, name="dw_win")
         nc.sync.dma_start(dw_win[:], d_words[0].rearrange("p n t -> p (n t)").bitcast(I32))
+        w_late = keep.tile([P, PACK, HALF], F32, name="w_late")
+        nc.sync.dma_start(w_late[:], w_rows[:, :, HALF:N])
         xw_win = keep.tile([P, T], I32, name="xw_win", tag="x_turn", align_bytes=64)
         nc.sync.dma_start(xw_win[:], x_words[0].rearrange("p n t -> p (n t)").bitcast(I32))
 
@@ -61,9 +60,10 @@ def tile_picked_scoremix_relu_p_kernel(tc, x_words, x_scales, d_words, d_scales,
         nc.scalar.activation(gn_half[:], gn_sb[:], ACT.Abs, scale=0.0625 * 0.5)
         nc.scalar.activation(gn_whole[:], gn_sb[:], ACT.Abs, scale=0.0625)
 
+        moved = keep.tile([P, H + S], U8, name="moved", align_bytes=64)
+        nc.vector.memset(moved[:].bitcast(I32), 0)
         ds_got = keep.tile([P, H], U8, name="ds_got")
         nc.vector.tensor_copy(ds_got[:], ds_win[:].indirect(kidx_sb[:]))
-
         both = keep.tile([P, H + S], U8, name="both")
         nc.vector.tensor_copy(
             both[:, 0:H].rearrange("p (t c i) -> p c t i", t=PACK, i=16),
@@ -72,16 +72,14 @@ def tile_picked_scoremix_relu_p_kernel(tc, x_words, x_scales, d_words, d_scales,
         xs_got = keep.tile([P, S], U8, name="xs_got")
         nc.vector.tensor_copy(xs_got[:], xs_win[:].indirect(offs_sb[:]))
         nc.vector.tensor_copy(both[:, H : H + S].bitcast(I32), xs_got[:].bitcast(I32))
-        placed = keep.tile([P, H + S], U8, name="placed", align_bytes=64)
-        nc.vector.tensor_copy(placed[:].bitcast(I32), both[:].bitcast(I32))
-        for e in range(2):
-            nc.sync.dma_start(placed[2 + e : P : 32, :].bitcast(I32), both[16 + e : P : 32, :].bitcast(I32))
+        for r in range(PACK):
+            nc.sync.dma_start(moved[r:P:32, :].bitcast(I32), both[8 * r : P : 32, :].bitcast(I32))
 
         w_grouped = keep.tile([P, N, PACK], BF16, name="w_grouped", align_bytes=64)
-        for a in range(2):
+        for a, raw in enumerate((w_early, w_late)):
             signed = keep.tile([P, PACK, HALF], BF16, name="w_signed%d" % a)
             for t in range(PACK):
-                nc.scalar.activation(signed[:, t, :], w_raw[a][:, t, :], ACT.Copy, scale=gn_sign[:, t : t + 1])
+                nc.scalar.activation(signed[:, t, :], raw[:, t, :], ACT.Copy, scale=gn_sign[:, t : t + 1])
             nc.scalar.copy(
                 w_grouped[:, a * HALF : (a + 1) * HALF, :].rearrange("p (c i) t -> p c t i", i=4),
                 signed[:].rearrange("p t (c i) -> p c t i", i=4),
@@ -101,13 +99,19 @@ def tile_picked_scoremix_relu_p_kernel(tc, x_words, x_scales, d_words, d_scales,
                 xw_win[:].bitcast(U32).indirect(offs_sb[:, h * 16 : (h + 1) * 16]),
             )
 
-        w_codes = keep.tile([P, N], U32, name="w_codes", tag="x_turn", align_bytes=64)
-        w_scales = keep.tile([P, N], U8, name="w_scales", align_bytes=64)
-        nc.vector.quantize_mx(
-            out=w_codes[:].bitcast(FP8X4), scales=w_scales[:], in_=w_grouped[:].rearrange("p m t -> p (m t)")
-        )
-
         out_rows = out.rearrange("(a p) j -> p a j", p=P)
+        w_codes = []
+        w_scales = []
+        for a, tag in enumerate(("w_first", "x_turn")):
+            codes = keep.tile([P, HALF], U32, name="w_codes%d" % a, tag=tag, align_bytes=64)
+            scales = keep.tile([P, HALF], U8, name="w_scales%d" % a, align_bytes=64)
+            nc.vector.quantize_mx(
+                out=codes[:].bitcast(FP8X4),
+                scales=scales[:],
+                in_=w_grouped[:, a * HALF : (a + 1) * HALF, :].rearrange("p m t -> p (m t)"),
+            )
+            w_codes.append(codes)
+            w_scales.append(scales)
 
         def mix(mixed, t, whole, j0, n):
             nc.vector.tensor_tensor(
@@ -115,7 +119,7 @@ def tile_picked_scoremix_relu_p_kernel(tc, x_words, x_scales, d_words, d_scales,
             )
 
         def rectify(mixed, n, engine, tag):
-            z = keep.tile([P, n, PACK], BF16, name="z_" + tag, tag=tag, align_bytes=64)
+            z = keep.tile([P, n, PACK], BF16, name="z_" + tag, align_bytes=64)
             dst = z[:].rearrange("p (c i) t -> p c t i", i=4)
             src = mixed[:].rearrange("p t (c i) -> p c t i", i=4)
             if engine is nc.scalar:
@@ -124,21 +128,26 @@ def tile_picked_scoremix_relu_p_kernel(tc, x_words, x_scales, d_words, d_scales,
                 nc.vector.tensor_scalar(dst, src, 0.0, None, ALU.max)
             return z
 
-        def project(z, j0, n, readers):
+        def quantise(z, j0, n):
             z_codes = keep.tile([P, n], U32, name="z_codes%d" % j0, align_bytes=64)
             z_scales = keep.tile([P, n], U8, name="z_scales%d" % j0, align_bytes=64)
             nc.vector.quantize_mx(
                 out=z_codes[:].bitcast(FP8X4), scales=z_scales[:], in_=z[:].rearrange("p j t -> p (j t)")
             )
+            return z_codes, z_scales
+
+        def project(z_mx, j0, n, readers):
+            z_codes, z_scales = z_mx
             blocks = 4 // len(readers)
             for r, engine in enumerate(readers):
                 acc = psum.tile([P, blocks, n], F32, name="acc2", tag="bank")
                 for a in range(blocks):
-                    m_cols = slice((r * blocks + a) * P, (r * blocks + a + 1) * P)
+                    half, block = divmod(r * blocks + a, 2)
+                    m_cols = slice(block * P, (block + 1) * P)
                     nc.tensor.matmul_mx(
                         out=acc[:, a, :],
-                        lhsT=w_codes[:, m_cols].bitcast(FP8X4),
-                        lhsT_scale=w_scales[:, m_cols],
+                        lhsT=w_codes[half][:, m_cols].bitcast(FP8X4),
+                        lhsT_scale=w_scales[half][:, m_cols],
                         rhs=z_codes[:].bitcast(FP8X4),
                         rhs_scale=z_scales[:],
                         start=True,
@@ -151,45 +160,51 @@ def tile_picked_scoremix_relu_p_kernel(tc, x_words, x_scales, d_words, d_scales,
                     nc.vector.tensor_copy(res[:], acc[:])
                 nc.sync.dma_start(out_rows[:, r * blocks : (r + 1) * blocks, j0 : j0 + n], res[:])
 
-        halved = []
-        right = []
-        mixed_a = keep.tile([P, PACK, HALF], F32, name="mixed_a")
+        halved = [keep.tile([P, S], F32, name="halved%d" % t) for t in range(PACK)]
+        left = [keep.tile([P, HALF], F32, name="left%d" % t) for t in range(PACK)]
+        mixed_a = keep.tile([P, PACK, HALF], F32, name="mixed_a", tag="mixed_turn")
+
+        def score(t, h):
+            cols = slice(h * HALF, (h + 1) * HALF)
+            acc = psum.tile([P, HALF], F32, name="acc", tag="bank")
+            nc.tensor.matmul_mx(
+                out=acc[:],
+                lhsT=d_codes[:, t, :].bitcast(FP8X4),
+                lhsT_scale=moved[:, t * P : (t + 1) * P],
+                rhs=x_codes[:, cols].bitcast(FP8X4),
+                rhs_scale=moved[:, H + h * HALF : H + (h + 1) * HALF],
+                start=True,
+                stop=True,
+            )
+            nc.scalar.activation(halved[t][:, cols], acc[:], ACT.Copy, scale=gn_half[:, t : t + 1])
+            return acc
+
+        def score_left(t):
+            score(t, 0)
+            nc.vector.tensor_scalar(left[t][:], halved[t][:, 0:HALF], 2.0, None, ALU.mult)
+
+        right_banks = []
+        score_left(0)
         for t in range(PACK):
-            row = keep.tile([P, S], F32, name="halved%d" % t)
-            left = keep.tile([P, HALF], F32, name="left%d" % t, tag="left%d" % t)
-            for h in range(2):
-                cols = slice(h * HALF, (h + 1) * HALF)
-                acc = psum.tile([P, HALF], F32, name="acc", tag="bank")
-                nc.tensor.matmul_mx(
-                    out=acc[:],
-                    lhsT=d_codes[:, t, :].bitcast(FP8X4),
-                    lhsT_scale=placed[:, t * P : (t + 1) * P],
-                    rhs=x_codes[:, cols].bitcast(FP8X4),
-                    rhs_scale=placed[:, H + h * HALF : H + (h + 1) * HALF],
-                    start=True,
-                    stop=True,
-                )
-                nc.scalar.activation(row[:, cols], acc[:], ACT.Copy, scale=gn_half[:, t : t + 1])
-                if h == 0:
-                    nc.scalar.activation(left[:], acc[:], ACT.Copy, scale=gn_whole[:, t : t + 1])
-            halved.append(row)
-            mix(mixed_a, t, left[:], 0, HALF)
+            if t + 1 < PACK:
+                score_left(t + 1)
+            right_banks.append(score(t, 1))
+            mix(mixed_a, t, left[t][:], 0, HALF)
+        right = []
+        for t in range(PACK):
             doubled = keep.tile([P, HALF], F32, name="right%d" % t)
-            if t < PACK - 1:
-                nc.vector.tensor_scalar(doubled[:], row[:, HALF:S], 2.0, None, ALU.mult)
-            else:
-                nc.scalar.activation(doubled[:], acc[:], ACT.Copy, scale=gn_whole[:, t : t + 1])
+            nc.scalar.activation(doubled[:], right_banks[t][:], ACT.Copy, scale=gn_whole[:, t : t + 1])
             right.append(doubled)
 
         z_a = rectify(mixed_a, HALF, nc.scalar, "a")
-        mixed_b = keep.tile([P, PACK, PIECE], F32, name="mixed_b", tag="left3")
+        mixed_b = keep.tile([P, PACK, PIECE], F32, name="mixed_b")
         for t in range(PACK):
             mix(mixed_b, t, right[t][:, 0:PIECE], HALF, PIECE)
         z_b = rectify(mixed_b, PIECE, nc.scalar, "b")
-        project(z_a, 0, HALF, (nc.scalar, nc.scalar))
-        mixed_c = keep.tile([P, PACK, PIECE], F32, name="mixed_c", tag="a", align_bytes=64)
+        project(quantise(z_a, 0, HALF), 0, HALF, (nc.scalar, nc.scalar))
+        mixed_c = keep.tile([P, PACK, PIECE], F32, name="mixed_c", tag="mixed_turn")
         for t in range(PACK):
             mix(mixed_c, t, right[t][:, PIECE:HALF], HALF + PIECE, PIECE)
-        project(z_b, HALF, PIECE, (nc.scalar,))
+        project(quantise(z_b, HALF, PIECE), HALF, PIECE, (nc.scalar,))
         z_c = rectify(mixed_c, PIECE, nc.vector, "c")
-        project(z_c, HALF + PIECE, PIECE, (nc.scalar, nc.vector))
+        project(quantise(z_c, HALF + PIECE, PIECE), HALF + PIECE, PIECE, (nc.scalar, nc.vector))

@@ -35,15 +35,15 @@ def tile_picked_scoremix_relu_p_kernel(tc, x_words, x_scales, d_words, d_scales,
         w_rows = w1.rearrange("(p t) m -> p t m", t=PACK)
         w_early = keep.tile([P, PACK, HALF], F32, name="w_early")
         nc.scalar.dma_start(w_early[:], w_rows[:, :, 0:HALF])
-        nc.scalar.dma_start(gn_sb[:], gn.rearrange("(p t) o -> p (t o)", t=PACK))
         nc.sync.dma_start(offs_sb[:], offs)
         nc.sync.dma_start(nb_sb[:], nb)
 
         ds_win = keep.tile([P, G], U8, name="ds_win")
         xs_win = keep.tile([P, T], U8, name="xs_win")
         nc.vector.memset(ds_win[:].bitcast(I32), 0)
-        nc.gpsimd.memset(xs_win[:].bitcast(I32), 0)
+        nc.vector.memset(xs_win[:].bitcast(I32), 0)
         nc.sync.dma_start(ds_win[0:P:8, :].bitcast(I32), d_scales[0].bitcast(I32))
+        nc.sync.dma_start(gn_sb[:], gn.rearrange("(p t) o -> p (t o)", t=PACK))
         nc.sync.dma_start(xs_win[0:P:8, :].bitcast(I32), x_scales[0].bitcast(I32))
 
         dw_win = keep.tile([P, G], I32, name="dw_win")
@@ -114,14 +114,12 @@ def tile_picked_scoremix_relu_p_kernel(tc, x_words, x_scales, d_words, d_scales,
             w_scales.append(scales)
 
         def mix(mixed, t, whole, j0, n):
-            nc.vector.tensor_tensor(
-                mixed[:, t, :], halved[t][:].indirect(nb_sb[:, j0 // 16 : (j0 + n) // 16]), whole, ALU.add
-            )
+            nc.vector.tensor_tensor(mixed, halved[t][:].indirect(nb_sb[:, j0 // 16 : (j0 + n) // 16]), whole, ALU.add)
 
         def rectify(mixed, n, engine, tag):
             z = keep.tile([P, n, PACK], BF16, name="z_" + tag, align_bytes=64)
             dst = z[:].rearrange("p (c i) t -> p c t i", i=4)
-            src = mixed[:].rearrange("p t (c i) -> p c t i", i=4)
+            src = mixed.rearrange("p t (c i) -> p c t i", i=4)
             if engine is nc.scalar:
                 nc.scalar.activation(dst, src, ACT.Relu)
             else:
@@ -136,33 +134,40 @@ def tile_picked_scoremix_relu_p_kernel(tc, x_words, x_scales, d_words, d_scales,
             )
             return z_codes, z_scales
 
-        def project(z_mx, j0, n, readers):
+        def product(z_mx, first, blocks, n):
             z_codes, z_scales = z_mx
-            blocks = 4 // len(readers)
-            for r, engine in enumerate(readers):
-                acc = psum.tile([P, blocks, n], F32, name="acc2", tag="bank")
-                for a in range(blocks):
-                    half, block = divmod(r * blocks + a, 2)
-                    m_cols = slice(block * P, (block + 1) * P)
-                    nc.tensor.matmul_mx(
-                        out=acc[:, a, :],
-                        lhsT=w_codes[half][:, m_cols].bitcast(FP8X4),
-                        lhsT_scale=w_scales[half][:, m_cols],
-                        rhs=z_codes[:].bitcast(FP8X4),
-                        rhs_scale=z_scales[:],
-                        start=True,
-                        stop=True,
-                    )
-                res = keep.tile([P, blocks, n], F32, name="res%d_%d" % (j0, r))
-                if engine is nc.scalar:
-                    nc.scalar.copy(res[:], acc[:])
-                else:
-                    nc.vector.tensor_copy(res[:], acc[:])
-                nc.sync.dma_start(out_rows[:, r * blocks : (r + 1) * blocks, j0 : j0 + n], res[:])
+            acc = psum.tile([P, blocks, n], F32, name="acc2", tag="bank")
+            for a in range(blocks):
+                half, block = divmod(first + a, 2)
+                m_cols = slice(block * P, (block + 1) * P)
+                nc.tensor.matmul_mx(
+                    out=acc[:, a, :],
+                    lhsT=w_codes[half][:, m_cols].bitcast(FP8X4),
+                    lhsT_scale=w_scales[half][:, m_cols],
+                    rhs=z_codes[:].bitcast(FP8X4),
+                    rhs_scale=z_scales[:],
+                    start=True,
+                    stop=True,
+                )
+            return acc
+
+        def project(z_mx, j0):
+            res = keep.tile([P, 4, PIECE], F32, name="res%d" % j0)
+            nc.scalar.copy(res[:], product(z_mx, 0, 4, PIECE)[:])
+            nc.sync.dma_start(out_rows[:, :, j0 : j0 + PIECE], res[:])
+
+        def project_last(z_mx, j0):
+            upper = keep.tile([P, 2, PIECE], F32, name="res_upper")
+            nc.scalar.copy(upper[:], product(z_mx, 0, 2, PIECE)[:])
+            nc.scalar.dma_start(out_rows[:, 0:2, j0 : j0 + PIECE], upper[:])
+            lower = keep.tile([P, 2, PIECE], F32, name="res_lower")
+            for a in range(2):
+                nc.vector.tensor_copy(lower[:, a : a + 1, :], product(z_mx, 2 + a, 1, PIECE)[:])
+            nc.sync.dma_start(out_rows[:, 2:4, j0 : j0 + PIECE], lower[:])
 
         halved = [keep.tile([P, S], F32, name="halved%d" % t) for t in range(PACK)]
         left = [keep.tile([P, HALF], F32, name="left%d" % t) for t in range(PACK)]
-        mixed_a = keep.tile([P, PACK, HALF], F32, name="mixed_a", tag="mixed_turn")
+        mixed_a = keep.tile([P, PACK, HALF], F32, name="mixed_a")
 
         def score(t, h):
             cols = slice(h * HALF, (h + 1) * HALF)
@@ -180,31 +185,43 @@ def tile_picked_scoremix_relu_p_kernel(tc, x_words, x_scales, d_words, d_scales,
             return acc
 
         def score_left(t):
-            score(t, 0)
-            nc.vector.tensor_scalar(left[t][:], halved[t][:, 0:HALF], 2.0, None, ALU.mult)
+            acc = score(t, 0)
+            if t < PACK - 1:
+                nc.vector.tensor_scalar(left[t][:], halved[t][:, 0:HALF], 2.0, None, ALU.mult)
+            return acc
+
+        def double_from_bank(dst, bank, t):
+            nc.scalar.activation(dst, bank, ACT.Copy, scale=gn_whole[:, t : t + 1])
 
         right_banks = []
         score_left(0)
         for t in range(PACK):
             if t + 1 < PACK:
-                score_left(t + 1)
+                left_bank = score_left(t + 1)
+            else:
+                double_from_bank(left[t][:], left_bank[:], t)
             right_banks.append(score(t, 1))
-            mix(mixed_a, t, left[t][:], 0, HALF)
+            mix(mixed_a[:, t, :], t, left[t][:], 0, HALF)
+
         right = []
         for t in range(PACK):
             doubled = keep.tile([P, HALF], F32, name="right%d" % t)
-            nc.scalar.activation(doubled[:], right_banks[t][:], ACT.Copy, scale=gn_whole[:, t : t + 1])
+            double_from_bank(doubled[:], right_banks[t][:], t)
             right.append(doubled)
 
-        z_a = rectify(mixed_a, HALF, nc.scalar, "a")
         mixed_b = keep.tile([P, PACK, PIECE], F32, name="mixed_b")
+        mixed_c = mixed_a[:, 0:2, :].rearrange("p a (b j) -> p (a b) j", j=PIECE)
+        z_0 = rectify(mixed_a[:, :, 0:PIECE], PIECE, nc.scalar, "0")
+        z_1 = rectify(mixed_a[:, :, PIECE:HALF], PIECE, nc.scalar, "1")
         for t in range(PACK):
-            mix(mixed_b, t, right[t][:, 0:PIECE], HALF, PIECE)
-        z_b = rectify(mixed_b, PIECE, nc.scalar, "b")
-        project(quantise(z_a, 0, HALF), 0, HALF, (nc.scalar, nc.scalar))
-        mixed_c = keep.tile([P, PACK, PIECE], F32, name="mixed_c", tag="mixed_turn")
-        for t in range(PACK):
-            mix(mixed_c, t, right[t][:, PIECE:HALF], HALF + PIECE, PIECE)
-        project(quantise(z_b, HALF, PIECE), HALF, PIECE, (nc.scalar,))
-        z_c = rectify(mixed_c, PIECE, nc.vector, "c")
-        project(quantise(z_c, HALF + PIECE, PIECE), HALF + PIECE, PIECE, (nc.scalar, nc.vector))
+            mix(mixed_b[:, t, :], t, right[t][:, 0:PIECE], HALF, PIECE)
+        z_2 = rectify(mixed_b[:], PIECE, nc.scalar, "2")
+        project(quantise(z_0, 0, PIECE), 0)
+        for t in (0, 2):
+            mix(mixed_c[:, t, :], t, right[t][:, PIECE:HALF], HALF + PIECE, PIECE)
+        project(quantise(z_1, PIECE, PIECE), PIECE)
+        for t in (1, 3):
+            mix(mixed_c[:, t, :], t, right[t][:, PIECE:HALF], HALF + PIECE, PIECE)
+        project(quantise(z_2, HALF, PIECE), HALF)
+        z_3 = rectify(mixed_c, PIECE, nc.vector, "3")
+        project_last(quantise(z_3, HALF + PIECE, PIECE), HALF + PIECE)

@@ -156,14 +156,17 @@ def tile_picked_scoremix_relu_p_kernel(tc, x_words, x_scales, d_words, d_scales,
             nc.scalar.copy(res[:], product(z_mx, 0, 4, PIECE)[:])
             nc.sync.dma_start(out_rows[:, :, j0 : j0 + PIECE], res[:])
 
-        def project_last(z_mx, j0):
-            upper = keep.tile([P, 2, PIECE], F32, name="res_upper")
-            nc.scalar.copy(upper[:], product(z_mx, 0, 2, PIECE)[:])
-            nc.scalar.dma_start(out_rows[:, 0:2, j0 : j0 + PIECE], upper[:])
-            lower = keep.tile([P, 2, PIECE], F32, name="res_lower")
-            for a in range(2):
-                nc.vector.tensor_copy(lower[:, a : a + 1, :], product(z_mx, 2 + a, 1, PIECE)[:])
-            nc.sync.dma_start(out_rows[:, 2:4, j0 : j0 + PIECE], lower[:])
+        def project_right(z_mx_b, z_mx_c):
+            res = keep.tile([P, 4, HALF], F32, name="res_right")
+            nc.scalar.copy(res[:, :, 0:PIECE], product(z_mx_b, 0, 4, PIECE)[:])
+            for a in range(4):
+                acc = product(z_mx_c, a, 1, PIECE)
+                if a % 2 == 1:
+                    nc.scalar.copy(res[:, a : a + 1, PIECE:HALF], acc[:])
+                    nc.scalar.dma_start(out_rows[:, a : a + 1, HALF:S], res[:, a : a + 1, :])
+                else:
+                    nc.vector.tensor_copy(res[:, a : a + 1, PIECE:HALF], acc[:])
+                    nc.sync.dma_start(out_rows[:, a : a + 1, HALF:S], res[:, a : a + 1, :])
 
         halved = [keep.tile([P, S], F32, name="halved%d" % t) for t in range(PACK)]
         left = [keep.tile([P, HALF], F32, name="left%d" % t) for t in range(PACK)]
@@ -222,6 +225,6 @@ def tile_picked_scoremix_relu_p_kernel(tc, x_words, x_scales, d_words, d_scales,
         project(quantise(z_1, PIECE, PIECE), PIECE)
         for t in (1, 3):
             mix(mixed_c[:, t, :], t, right[t][:, PIECE:HALF], HALF + PIECE, PIECE)
-        project(quantise(z_2, HALF, PIECE), HALF)
+        z_2_mx = quantise(z_2, HALF, PIECE)
         z_3 = rectify(mixed_c, PIECE, nc.vector, "3")
-        project_last(quantise(z_3, HALF + PIECE, PIECE), HALF + PIECE)
+        project_right(z_2_mx, quantise(z_3, HALF + PIECE, PIECE))

@@ -33,8 +33,8 @@ def tile_picked_scoremix_relu_p_kernel(tc, x_words, x_scales, d_words, d_scales,
         gn_sb = keep.tile([P, PACK], F32, name="gn_sb")
         nc.sync.dma_start(kidx_sb[:], kidx)
         w_rows = w1.rearrange("(p t) m -> p t m", t=PACK)
-        w_early = keep.tile([P, PACK, HALF], F32, name="w_early")
-        nc.scalar.dma_start(w_early[:], w_rows[:, :, 0:HALF])
+        w_early = keep.tile([P, 2, N], F32, name="w_early")
+        nc.scalar.dma_start(w_early[:], w_rows[:, 0:2, :])
         nc.sync.dma_start(offs_sb[:], offs)
         nc.sync.dma_start(nb_sb[:], nb)
 
@@ -48,8 +48,8 @@ def tile_picked_scoremix_relu_p_kernel(tc, x_words, x_scales, d_words, d_scales,
 
         dw_win = keep.tile([P, G], I32, name="dw_win")
         nc.sync.dma_start(dw_win[:], d_words[0].rearrange("p n t -> p (n t)").bitcast(I32))
-        w_late = keep.tile([P, PACK, HALF], F32, name="w_late")
-        nc.sync.dma_start(w_late[:], w_rows[:, :, HALF:N])
+        w_late = keep.tile([P, 2, N], F32, name="w_late")
+        nc.sync.dma_start(w_late[:], w_rows[:, 2:PACK, :])
         xw_win = keep.tile([P, T], I32, name="xw_win", tag="x_turn", align_bytes=64)
         nc.sync.dma_start(xw_win[:], x_words[0].rearrange("p n t -> p (n t)").bitcast(I32))
 
@@ -76,14 +76,16 @@ def tile_picked_scoremix_relu_p_kernel(tc, x_words, x_scales, d_words, d_scales,
             nc.sync.dma_start(moved[r:P:32, :].bitcast(I32), both[8 * r : P : 32, :].bitcast(I32))
 
         w_grouped = keep.tile([P, N, PACK], BF16, name="w_grouped", align_bytes=64)
-        for a, raw in enumerate((w_early, w_late)):
-            signed = keep.tile([P, PACK, HALF], BF16, name="w_signed%d" % a)
-            for t in range(PACK):
-                nc.scalar.activation(signed[:, t, :], raw[:, t, :], ACT.Copy, scale=gn_sign[:, t : t + 1])
-            nc.scalar.copy(
-                w_grouped[:, a * HALF : (a + 1) * HALF, :].rearrange("p (c i) t -> p c t i", i=4),
-                signed[:].rearrange("p t (c i) -> p c t i", i=4),
-            )
+        w_pairs = keep.tile([P, 2, N, 2], BF16, name="w_pairs")
+        for u, raw in enumerate((w_early, w_late)):
+            for e in range(2):
+                t = 2 * u + e
+                nc.scalar.activation(w_pairs[:, u, :, e], raw[:, e, :], ACT.Copy, scale=gn_sign[:, t : t + 1])
+        pair_words = w_pairs[:].rearrange("p u m e -> p u (m e)").bitcast(U32)
+        grouped_words = w_grouped[:].rearrange("p m t -> p (m t)").bitcast(U32).rearrange("p (m u) -> p m u", u=2)
+        nc.scalar.copy(
+            grouped_words.rearrange("p (c i) u -> p c u i", i=4), pair_words.rearrange("p u (c i) -> p c u i", i=4)
+        )
 
         dw_got = keep.tile([P, H], U32, name="dw_got")
         nc.vector.tensor_copy(dw_got[:], dw_win[:].bitcast(U32).indirect(kidx_sb[:]))
@@ -100,18 +102,11 @@ def tile_picked_scoremix_relu_p_kernel(tc, x_words, x_scales, d_words, d_scales,
             )
 
         out_rows = out.rearrange("(a p) j -> p a j", p=P)
-        w_codes = []
-        w_scales = []
-        for a, tag in enumerate(("w_first", "x_turn")):
-            codes = keep.tile([P, HALF], U32, name="w_codes%d" % a, tag=tag, align_bytes=64)
-            scales = keep.tile([P, HALF], U8, name="w_scales%d" % a, align_bytes=64)
-            nc.vector.quantize_mx(
-                out=codes[:].bitcast(FP8X4),
-                scales=scales[:],
-                in_=w_grouped[:, a * HALF : (a + 1) * HALF, :].rearrange("p m t -> p (m t)"),
-            )
-            w_codes.append(codes)
-            w_scales.append(scales)
+        w_codes = keep.tile([P, N], U32, name="w_codes", tag="x_turn", align_bytes=64)
+        w_scales = keep.tile([P, N], U8, name="w_scales", align_bytes=64)
+        nc.vector.quantize_mx(
+            out=w_codes[:].bitcast(FP8X4), scales=w_scales[:], in_=w_grouped[:].rearrange("p m t -> p (m t)")
+        )
 
         def mix(mixed, t, whole, j0, n):
             nc.vector.tensor_tensor(mixed, halved[t][:].indirect(nb_sb[:, j0 // 16 : (j0 + n) // 16]), whole, ALU.add)
@@ -138,12 +133,11 @@ def tile_picked_scoremix_relu_p_kernel(tc, x_words, x_scales, d_words, d_scales,
             z_codes, z_scales = z_mx
             acc = psum.tile([P, blocks, n], F32, name="acc2", tag="bank")
             for a in range(blocks):
-                half, block = divmod(first + a, 2)
-                m_cols = slice(block * P, (block + 1) * P)
+                m_cols = slice((first + a) * P, (first + a + 1) * P)
                 nc.tensor.matmul_mx(
                     out=acc[:, a, :],
-                    lhsT=w_codes[half][:, m_cols].bitcast(FP8X4),
-                    lhsT_scale=w_scales[half][:, m_cols],
+                    lhsT=w_codes[:, m_cols].bitcast(FP8X4),
+                    lhsT_scale=w_scales[:, m_cols],
                     rhs=z_codes[:].bitcast(FP8X4),
                     rhs_scale=z_scales[:],
                     start=True,
@@ -152,9 +146,10 @@ def tile_picked_scoremix_relu_p_kernel(tc, x_words, x_scales, d_words, d_scales,
             return acc
 
         def project(z_mx, j0):
-            res = keep.tile([P, 4, PIECE], F32, name="res%d" % j0)
-            nc.scalar.copy(res[:], product(z_mx, 0, 4, PIECE)[:])
-            nc.sync.dma_start(out_rows[:, :, j0 : j0 + PIECE], res[:])
+            for first in (0, 2):
+                res = keep.tile([P, 2, PIECE], F32, name="res%d_%d" % (j0, first))
+                nc.scalar.copy(res[:], product(z_mx, first, 2, PIECE)[:])
+                nc.sync.dma_start(out_rows[:, first : first + 2, j0 : j0 + PIECE], res[:])
 
         def project_right(z_mx_b, z_mx_c):
             res = keep.tile([P, 4, HALF], F32, name="res_right")

@@ -152,16 +152,20 @@ def tile_picked_scoremix_relu_p_kernel(tc, x_words, x_scales, d_words, d_scales,
                 nc.sync.dma_start(out_rows[:, first : first + 2, j0 : j0 + PIECE], res[:])
 
         def project_right(z_mx_b, z_mx_c):
+            early = keep.tile([P, 2, PIECE], F32, name="res_early")
+            nc.scalar.copy(early[:], product(z_mx_b, 2, 2, PIECE)[:])
+            nc.sync.dma_start(out_rows[:, 2:4, HALF : HALF + PIECE], early[:])
             res = keep.tile([P, 4, HALF], F32, name="res_right")
-            nc.scalar.copy(res[:, :, 0:PIECE], product(z_mx_b, 0, 4, PIECE)[:])
+            nc.scalar.copy(res[:, 0:2, 0:PIECE], product(z_mx_b, 0, 2, PIECE)[:])
             for a in range(4):
                 acc = product(z_mx_c, a, 1, PIECE)
+                first = 0 if a < 2 else PIECE
                 if a % 2 == 1:
                     nc.scalar.copy(res[:, a : a + 1, PIECE:HALF], acc[:])
-                    nc.scalar.dma_start(out_rows[:, a : a + 1, HALF:S], res[:, a : a + 1, :])
+                    nc.scalar.dma_start(out_rows[:, a : a + 1, HALF + first : S], res[:, a : a + 1, first:HALF])
                 else:
                     nc.vector.tensor_copy(res[:, a : a + 1, PIECE:HALF], acc[:])
-                    nc.sync.dma_start(out_rows[:, a : a + 1, HALF:S], res[:, a : a + 1, :])
+                    nc.sync.dma_start(out_rows[:, a : a + 1, HALF + first : S], res[:, a : a + 1, first:HALF])
 
         halved = [keep.tile([P, S], F32, name="halved%d" % t) for t in range(PACK)]
         left = [keep.tile([P, HALF], F32, name="left%d" % t) for t in range(PACK)]

@@ -33,25 +33,25 @@ def tile_picked_scoremix_relu_p_kernel(tc, x_words, x_scales, d_words, d_scales,
         gn_sb = keep.tile([P, PACK], F32, name="gn_sb")
         nc.sync.dma_start(kidx_sb[:], kidx)
         w_rows = w1.rearrange("(p t) m -> p t m", t=PACK)
-        w_early = keep.tile([P, 2, N], F32, name="w_early")
+        w_early = keep.tile([P, 2, N], F32, name="w_early", tag="w_turn")
         nc.scalar.dma_start(w_early[:], w_rows[:, 0:2, :])
         nc.sync.dma_start(offs_sb[:], offs)
-        nc.sync.dma_start(nb_sb[:], nb)
+        nc.sync.dma_start(gn_sb[:], gn.rearrange("(p t) o -> p (t o)", t=PACK))
 
         ds_win = keep.tile([P, G], U8, name="ds_win")
         xs_win = keep.tile([P, T], U8, name="xs_win")
         nc.vector.memset(ds_win[:].bitcast(I32), 0)
         nc.vector.memset(xs_win[:].bitcast(I32), 0)
         nc.sync.dma_start(ds_win[0:P:8, :].bitcast(I32), d_scales[0].bitcast(I32))
-        nc.sync.dma_start(gn_sb[:], gn.rearrange("(p t) o -> p (t o)", t=PACK))
+        w_late = keep.tile([P, 2, N], F32, name="w_late")
+        nc.sync.dma_start(w_late[:], w_rows[:, 2:PACK, :])
         nc.sync.dma_start(xs_win[0:P:8, :].bitcast(I32), x_scales[0].bitcast(I32))
 
         dw_win = keep.tile([P, G], I32, name="dw_win")
         nc.sync.dma_start(dw_win[:], d_words[0].rearrange("p n t -> p (n t)").bitcast(I32))
-        w_late = keep.tile([P, 2, N], F32, name="w_late")
-        nc.sync.dma_start(w_late[:], w_rows[:, 2:PACK, :])
         xw_win = keep.tile([P, T], I32, name="xw_win", tag="x_turn", align_bytes=64)
         nc.sync.dma_start(xw_win[:], x_words[0].rearrange("p n t -> p (n t)").bitcast(I32))
+        nc.sync.dma_start(nb_sb[:], nb)
 
         gn_sign = keep.tile([P, PACK], F32, name="gn_sign")
         gn_half = keep.tile([P, PACK], F32, name="gn_half")
@@ -59,21 +59,6 @@ def tile_picked_scoremix_relu_p_kernel(tc, x_words, x_scales, d_words, d_scales,
         nc.scalar.activation(gn_sign[:], gn_sb[:], ACT.Sign)
         nc.scalar.activation(gn_half[:], gn_sb[:], ACT.Abs, scale=0.0625 * 0.5)
         nc.scalar.activation(gn_whole[:], gn_sb[:], ACT.Abs, scale=0.0625)
-
-        moved = keep.tile([P, H + S], U8, name="moved", align_bytes=64)
-        nc.vector.memset(moved[:].bitcast(I32), 0)
-        ds_got = keep.tile([P, H], U8, name="ds_got")
-        nc.vector.tensor_copy(ds_got[:], ds_win[:].indirect(kidx_sb[:]))
-        both = keep.tile([P, H + S], U8, name="both")
-        nc.vector.tensor_copy(
-            both[:, 0:H].rearrange("p (t c i) -> p c t i", t=PACK, i=16),
-            ds_got[:].rearrange("p (c i t) -> p c t i", t=PACK, i=16),
-        )
-        xs_got = keep.tile([P, S], U8, name="xs_got")
-        nc.vector.tensor_copy(xs_got[:], xs_win[:].indirect(offs_sb[:]))
-        nc.vector.tensor_copy(both[:, H : H + S].bitcast(I32), xs_got[:].bitcast(I32))
-        for r in range(PACK):
-            nc.sync.dma_start(moved[r:P:32, :].bitcast(I32), both[8 * r : P : 32, :].bitcast(I32))
 
         w_grouped = keep.tile([P, N, PACK], BF16, name="w_grouped", align_bytes=64)
         w_pairs = keep.tile([P, 2, N, 2], BF16, name="w_pairs")
@@ -86,6 +71,21 @@ def tile_picked_scoremix_relu_p_kernel(tc, x_words, x_scales, d_words, d_scales,
         nc.scalar.copy(
             grouped_words.rearrange("p (c i) u -> p c u i", i=4), pair_words.rearrange("p u (c i) -> p c u i", i=4)
         )
+
+        moved = keep.tile([P, H + S], U8, name="moved", align_bytes=64)
+        nc.vector.memset(moved[:].bitcast(I32), 0)
+        ds_got = keep.tile([P, H], U8, name="ds_got")
+        nc.vector.tensor_copy(ds_got[:], ds_win[:].indirect(kidx_sb[:]))
+        xs_got = keep.tile([P, S], U8, name="xs_got")
+        nc.vector.tensor_copy(xs_got[:], xs_win[:].indirect(offs_sb[:]))
+        both = keep.tile([P, H + S], U8, name="both", tag="w_turn")
+        nc.vector.tensor_copy(
+            both[:, 0:H].rearrange("p (t c i) -> p c t i", t=PACK, i=16),
+            ds_got[:].rearrange("p (c i t) -> p c t i", t=PACK, i=16),
+        )
+        nc.vector.tensor_copy(both[:, H : H + S].bitcast(I32), xs_got[:].bitcast(I32))
+        for r in range(PACK):
+            nc.sync.dma_start(moved[r:P:32, :].bitcast(I32), both[8 * r : P : 32, :].bitcast(I32))
 
         dw_got = keep.tile([P, H], U32, name="dw_got")
         nc.vector.tensor_copy(dw_got[:], dw_win[:].bitcast(U32).indirect(kidx_sb[:]))

@@ -33,7 +33,7 @@ def tile_picked_scoremix_relu_p_kernel(tc, x_words, x_scales, d_words, d_scales,
         gn_sb = keep.tile([P, PACK], F32, name="gn_sb")
         nc.sync.dma_start(kidx_sb[:], kidx)
         w_rows = w1.rearrange("(p t) m -> p t m", t=PACK)
-        w_early = keep.tile([P, 2, N], F32, name="w_early", tag="w_turn")
+        w_early = keep.tile([P, 2, N], F32, name="w_early", tag="w_turn", align_bytes=64)
         nc.scalar.dma_start(w_early[:], w_rows[:, 0:2, :])
         nc.sync.dma_start(offs_sb[:], offs)
         nc.sync.dma_start(gn_sb[:], gn.rearrange("(p t) o -> p (t o)", t=PACK))
@@ -62,30 +62,31 @@ def tile_picked_scoremix_relu_p_kernel(tc, x_words, x_scales, d_words, d_scales,
 
         w_grouped = keep.tile([P, N, PACK], BF16, name="w_grouped", align_bytes=64)
         w_pairs = keep.tile([P, 2, N, 2], BF16, name="w_pairs")
-        for u, raw in enumerate((w_early, w_late)):
+
+        def sign_rows(u, raw):
             for e in range(2):
                 t = 2 * u + e
                 nc.scalar.activation(w_pairs[:, u, :, e], raw[:, e, :], ACT.Copy, scale=gn_sign[:, t : t + 1])
+
+        sign_rows(0, w_early)
+        ds_got = keep.tile([P, H], U8, name="ds_got")
+        nc.vector.tensor_copy(ds_got[:], ds_win[:].indirect(kidx_sb[:]))
+        xs_got = keep.tile([P, S], U8, name="xs_got")
+        nc.vector.tensor_copy(xs_got[:], xs_win[:].indirect(offs_sb[:]))
+        moved = keep.tile([P, H + S], U8, name="moved", tag="w_turn", align_bytes=64)
+        nc.vector.tensor_copy(
+            moved[:, 0:H].rearrange("p (t c i) -> p c t i", t=PACK, i=16),
+            ds_got[:].rearrange("p (c i t) -> p c t i", t=PACK, i=16),
+        )
+        nc.vector.tensor_copy(moved[:, H : H + S].bitcast(I32), xs_got[:].bitcast(I32))
+        for r in range(1, PACK):
+            nc.scalar.dma_start(moved[r:P:32, :].bitcast(I32), moved[8 * r : P : 32, :].bitcast(I32))
+        sign_rows(1, w_late)
         pair_words = w_pairs[:].rearrange("p u m e -> p u (m e)").bitcast(U32)
         grouped_words = w_grouped[:].rearrange("p m t -> p (m t)").bitcast(U32).rearrange("p (m u) -> p m u", u=2)
         nc.scalar.copy(
             grouped_words.rearrange("p (c i) u -> p c u i", i=4), pair_words.rearrange("p u (c i) -> p c u i", i=4)
         )
-
-        moved = keep.tile([P, H + S], U8, name="moved", align_bytes=64)
-        nc.vector.memset(moved[:].bitcast(I32), 0)
-        ds_got = keep.tile([P, H], U8, name="ds_got")
-        nc.vector.tensor_copy(ds_got[:], ds_win[:].indirect(kidx_sb[:]))
-        xs_got = keep.tile([P, S], U8, name="xs_got")
-        nc.vector.tensor_copy(xs_got[:], xs_win[:].indirect(offs_sb[:]))
-        both = keep.tile([P, H + S], U8, name="both", tag="w_turn")
-        nc.vector.tensor_copy(
-            both[:, 0:H].rearrange("p (t c i) -> p c t i", t=PACK, i=16),
-            ds_got[:].rearrange("p (c i t) -> p c t i", t=PACK, i=16),
-        )
-        nc.vector.tensor_copy(both[:, H : H + S].bitcast(I32), xs_got[:].bitcast(I32))
-        for r in range(PACK):
-            nc.sync.dma_start(moved[r:P:32, :].bitcast(I32), both[8 * r : P : 32, :].bitcast(I32))
 
         dw_got = keep.tile([P, H], U32, name="dw_got")
         nc.vector.tensor_copy(dw_got[:], dw_win[:].bitcast(U32).indirect(kidx_sb[:]))
@@ -159,13 +160,13 @@ def tile_picked_scoremix_relu_p_kernel(tc, x_words, x_scales, d_words, d_scales,
             nc.scalar.copy(res[:, 0:2, 0:PIECE], product(z_mx_b, 0, 2, PIECE)[:])
             for a in range(4):
                 acc = product(z_mx_c, a, 1, PIECE)
-                first = 0 if a < 2 else PIECE
                 if a % 2 == 1:
                     nc.scalar.copy(res[:, a : a + 1, PIECE:HALF], acc[:])
-                    nc.scalar.dma_start(out_rows[:, a : a + 1, HALF + first : S], res[:, a : a + 1, first:HALF])
                 else:
                     nc.vector.tensor_copy(res[:, a : a + 1, PIECE:HALF], acc[:])
-                    nc.sync.dma_start(out_rows[:, a : a + 1, HALF + first : S], res[:, a : a + 1, first:HALF])
+                if a < 2:
+                    nc.sync.dma_start(out_rows[:, a : a + 1, HALF:S], res[:, a : a + 1, :])
+            nc.scalar.dma_start(out_rows[:, 2:4, HALF + PIECE : S], res[:, 2:4, PIECE:HALF])
 
         halved = [keep.tile([P, S], F32, name="halved%d" % t) for t in range(PACK)]
         left = [keep.tile([P, HALF], F32, name="left%d" % t) for t in range(PACK)]

@@ -114,8 +114,8 @@ def tile_picked_scoremix_relu_p_kernel(tc, x_words, x_scales, d_words, d_scales,
 
         def rectify(mixed, n, engine, tag):
             z = keep.tile([P, n, PACK], BF16, name="z_" + tag, align_bytes=64)
-            dst = z[:].rearrange("p (c i) t -> p c t i", i=4)
-            src = mixed.rearrange("p t (c i) -> p c t i", i=4)
+            dst = z[:].rearrange("p (c i) t -> p c t i", i=2)
+            src = mixed.rearrange("p t (c i) -> p c t i", i=2)
             if engine is nc.scalar:
                 nc.scalar.activation(dst, src, ACT.Relu)
             else:
@@ -172,44 +172,39 @@ def tile_picked_scoremix_relu_p_kernel(tc, x_words, x_scales, d_words, d_scales,
         left = [keep.tile([P, HALF], F32, name="left%d" % t) for t in range(PACK)]
         mixed_a = keep.tile([P, PACK, HALF], F32, name="mixed_a")
 
-        def score(t, h):
-            cols = slice(h * HALF, (h + 1) * HALF)
-            acc = psum.tile([P, HALF], F32, name="acc", tag="bank")
+        def score(t, j0, n):
+            acc = psum.tile([P, n], F32, name="acc", tag="bank")
             nc.tensor.matmul_mx(
                 out=acc[:],
                 lhsT=d_codes[:, t, :].bitcast(FP8X4),
                 lhsT_scale=moved[:, t * P : (t + 1) * P],
-                rhs=x_codes[:, cols].bitcast(FP8X4),
-                rhs_scale=moved[:, H + h * HALF : H + (h + 1) * HALF],
+                rhs=x_codes[:, j0 : j0 + n].bitcast(FP8X4),
+                rhs_scale=moved[:, H + j0 : H + j0 + n],
                 start=True,
                 stop=True,
             )
-            nc.scalar.activation(halved[t][:, cols], acc[:], ACT.Copy, scale=gn_half[:, t : t + 1])
+            nc.scalar.activation(halved[t][:, j0 : j0 + n], acc[:], ACT.Copy, scale=gn_half[:, t : t + 1])
             return acc
 
         def score_left(t):
-            acc = score(t, 0)
-            if t < PACK - 1:
-                nc.vector.tensor_scalar(left[t][:], halved[t][:, 0:HALF], 2.0, None, ALU.mult)
-            return acc
+            score(t, 0, HALF)
+            nc.vector.tensor_scalar(left[t][:], halved[t][:, 0:HALF], 2.0, None, ALU.mult)
 
-        def double_from_bank(dst, bank, t):
-            nc.scalar.activation(dst, bank, ACT.Copy, scale=gn_whole[:, t : t + 1])
-
-        right_banks = []
+        last = PACK - 1
         score_left(0)
-        for t in range(PACK):
-            if t + 1 < PACK:
-                left_bank = score_left(t + 1)
-            else:
-                double_from_bank(left[t][:], left_bank[:], t)
-            right_banks.append(score(t, 1))
+        for t in range(last):
+            if t + 1 < last:
+                score_left(t + 1)
+            score(t, HALF, HALF)
             mix(mixed_a[:, t, :], t, left[t][:], 0, HALF)
+        bank = score(last, 0, S)
+        nc.scalar.activation(left[last][:], bank[:, 0:HALF], ACT.Copy, scale=gn_whole[:, last : last + 1])
+        mix(mixed_a[:, last, :], last, left[last][:], 0, HALF)
 
         right = []
         for t in range(PACK):
             doubled = keep.tile([P, HALF], F32, name="right%d" % t)
-            double_from_bank(doubled[:], right_banks[t][:], t)
+            nc.scalar.activation(doubled[:], halved[t][:, HALF:S], ACT.Copy, scale=2.0)
             right.append(doubled)
 
         mixed_b = keep.tile([P, PACK, PIECE], F32, name="mixed_b")

@@ -31,15 +31,15 @@ def tile_picked_scoremix_relu_p_kernel(tc, x_words, x_scales, d_words, d_scales,
         offs_sb = keep.tile([P, S // 16], U16, name="offs_sb")
         nb_sb = keep.tile([P, S // 16], U16, name="nb_sb")
         gn_sb = keep.tile([P, PACK], F32, name="gn_sb")
+        nc.sync.dma_start(gn_sb[:], gn.rearrange("(p t) o -> p (t o)", t=PACK))
         nc.sync.dma_start(kidx_sb[:], kidx)
         w_rows = w1.rearrange("(p t) m -> p t m", t=PACK)
-        w_early = keep.tile([P, 2, N], F32, name="w_early", tag="w_turn", align_bytes=64)
+        w_early = keep.tile([P, 2, N], F32, name="w_early")
         nc.scalar.dma_start(w_early[:], w_rows[:, 0:2, :])
         nc.sync.dma_start(offs_sb[:], offs)
-        nc.sync.dma_start(gn_sb[:], gn.rearrange("(p t) o -> p (t o)", t=PACK))
 
         ds_win = keep.tile([P, G], U8, name="ds_win")
-        xs_win = keep.tile([P, T], U8, name="xs_win")
+        xs_win = keep.tile([P, T], U8, name="xs_win", tag="window_turn", align_bytes=64)
         nc.vector.memset(ds_win[:].bitcast(I32), 0)
         nc.vector.memset(xs_win[:].bitcast(I32), 0)
         nc.sync.dma_start(ds_win[0:P:8, :].bitcast(I32), d_scales[0].bitcast(I32))
@@ -73,7 +73,7 @@ def tile_picked_scoremix_relu_p_kernel(tc, x_words, x_scales, d_words, d_scales,
         nc.vector.tensor_copy(ds_got[:], ds_win[:].indirect(kidx_sb[:]))
         xs_got = keep.tile([P, S], U8, name="xs_got")
         nc.vector.tensor_copy(xs_got[:], xs_win[:].indirect(offs_sb[:]))
-        moved = keep.tile([P, H + S], U8, name="moved", tag="w_turn", align_bytes=64)
+        moved = keep.tile([P, H + S], U8, name="moved", tag="window_turn", align_bytes=64)
         nc.vector.tensor_copy(
             moved[:, 0:H].rearrange("p (t c i) -> p c t i", t=PACK, i=16),
             ds_got[:].rearrange("p (c i t) -> p c t i", t=PACK, i=16),

@@ -96,10 +96,9 @@ def tile_picked_scoremix_relu_p_kernel(tc, x_words, x_scales, d_words, d_scales,
         )
 
         x_codes = keep.tile([P, S], U32, name="x_codes", align_bytes=64)
-        for h in range(2):
+        for j0, n in ((0, PIECE), (PIECE, PIECE), (HALF, HALF)):
             nc.vector.tensor_copy(
-                x_codes[:, h * HALF : (h + 1) * HALF],
-                xw_win[:].bitcast(U32).indirect(offs_sb[:, h * 16 : (h + 1) * 16]),
+                x_codes[:, j0 : j0 + n], xw_win[:].bitcast(U32).indirect(offs_sb[:, j0 // 16 : (j0 + n) // 16])
             )
 
         out_rows = out.rearrange("(a p) j -> p a j", p=P)
@@ -186,15 +185,15 @@ def tile_picked_scoremix_relu_p_kernel(tc, x_words, x_scales, d_words, d_scales,
             nc.scalar.activation(halved[t][:, j0 : j0 + n], acc[:], ACT.Copy, scale=gn_half[:, t : t + 1])
             return acc
 
-        def score_left(t):
-            score(t, 0, HALF)
-            nc.vector.tensor_scalar(left[t][:], halved[t][:, 0:HALF], 2.0, None, ALU.mult)
-
         last = PACK - 1
-        score_left(0)
+        for t in range(2):
+            score(t, 0, PIECE)
+        for t in range(2):
+            score(t, PIECE, PIECE)
+            nc.vector.tensor_scalar(left[t][:], halved[t][:, 0:HALF], 2.0, None, ALU.mult)
+        score(2, 0, HALF)
+        nc.vector.tensor_scalar(left[2][:], halved[2][:, 0:HALF], 2.0, None, ALU.mult)
         for t in range(last):
-            if t + 1 < last:
-                score_left(t + 1)
             score(t, HALF, HALF)
             mix(mixed_a[:, t, :], t, left[t][:], 0, HALF)
         bank = score(last, 0, S)

@@ -19,6 +19,7 @@ P = 128
 PACK = 4
 HALF = 256
 PIECE = 128
+BURST = 256
 
 
 def tile_picked_scoremix_relu_p_kernel(tc, x_words, x_scales, d_words, d_scales, gn, w1, offs, kidx, nb, out):
@@ -34,22 +35,22 @@ def tile_picked_scoremix_relu_p_kernel(tc, x_words, x_scales, d_words, d_scales,
         nc.sync.dma_start(gn_sb[:], gn.rearrange("(p t) o -> p (t o)", t=PACK))
         nc.sync.dma_start(kidx_sb[:], kidx)
         w_rows = w1.rearrange("(p t) m -> p t m", t=PACK)
-        w_early = keep.tile([P, 2, N], F32, name="w_early")
+        w_early = keep.tile([P, 2, N], F32, name="w_early", align_bytes=BURST)
         nc.scalar.dma_start(w_early[:], w_rows[:, 0:2, :])
         nc.sync.dma_start(offs_sb[:], offs)
 
-        ds_win = keep.tile([P, G], U8, name="ds_win")
-        xs_win = keep.tile([P, T], U8, name="xs_win", tag="window_turn", align_bytes=64)
+        ds_win = keep.tile([P, G], U8, name="ds_win", align_bytes=BURST)
+        xs_win = keep.tile([P, T], U8, name="xs_win", tag="window_turn", align_bytes=BURST)
         nc.vector.memset(ds_win[:].bitcast(I32), 0)
         nc.vector.memset(xs_win[:].bitcast(I32), 0)
         nc.sync.dma_start(ds_win[0:P:8, :].bitcast(I32), d_scales[0].bitcast(I32))
-        w_late = keep.tile([P, 2, N], F32, name="w_late")
+        w_late = keep.tile([P, 2, N], F32, name="w_late", align_bytes=BURST)
         nc.sync.dma_start(w_late[:], w_rows[:, 2:PACK, :])
         nc.sync.dma_start(xs_win[0:P:8, :].bitcast(I32), x_scales[0].bitcast(I32))
 
-        dw_win = keep.tile([P, G], I32, name="dw_win")
+        dw_win = keep.tile([P, G], I32, name="dw_win", align_bytes=BURST)
         nc.sync.dma_start(dw_win[:], d_words[0].rearrange("p n t -> p (n t)").bitcast(I32))
-        xw_win = keep.tile([P, T], I32, name="xw_win", tag="x_turn", align_bytes=64)
+        xw_win = keep.tile([P, T], I32, name="xw_win", tag="x_turn", align_bytes=BURST)
         nc.sync.dma_start(xw_win[:], x_words[0].rearrange("p n t -> p (n t)").bitcast(I32))
         nc.sync.dma_start(nb_sb[:], nb)
 
@@ -73,7 +74,7 @@ def tile_picked_scoremix_relu_p_kernel(tc, x_words, x_scales, d_words, d_scales,
         nc.vector.tensor_copy(ds_got[:], ds_win[:].indirect(kidx_sb[:]))
         xs_got = keep.tile([P, S], U8, name="xs_got")
         nc.vector.tensor_copy(xs_got[:], xs_win[:].indirect(offs_sb[:]))
-        moved = keep.tile([P, H + S], U8, name="moved", tag="window_turn", align_bytes=64)
+        moved = keep.tile([P, H + S], U8, name="moved", tag="window_turn", align_bytes=BURST)
         nc.vector.tensor_copy(
             moved[:, 0:H].rearrange("p (t c i) -> p c t i", t=PACK, i=16),
             ds_got[:].rearrange("p (c i t) -> p c t i", t=PACK, i=16),
@@ -102,7 +103,7 @@ def tile_picked_scoremix_relu_p_kernel(tc, x_words, x_scales, d_words, d_scales,
             )
 
         out_rows = out.rearrange("(a p) j -> p a j", p=P)
-        w_codes = keep.tile([P, N], U32, name="w_codes", tag="x_turn", align_bytes=64)
+        w_codes = keep.tile([P, N], U32, name="w_codes", tag="x_turn", align_bytes=BURST)
         w_scales = keep.tile([P, N], U8, name="w_scales", align_bytes=64)
         nc.vector.quantize_mx(
             out=w_codes[:].bitcast(FP8X4), scales=w_scales[:], in_=w_grouped[:].rearrange("p m t -> p (m t)")
@@ -147,15 +148,15 @@ def tile_picked_scoremix_relu_p_kernel(tc, x_words, x_scales, d_words, d_scales,
 
         def project(z_mx, j0):
             for first in (0, 2):
-                res = keep.tile([P, 2, PIECE], F32, name="res%d_%d" % (j0, first))
+                res = keep.tile([P, 2, PIECE], F32, name="res%d_%d" % (j0, first), align_bytes=BURST)
                 nc.scalar.copy(res[:], product(z_mx, first, 2, PIECE)[:])
                 nc.sync.dma_start(out_rows[:, first : first + 2, j0 : j0 + PIECE], res[:])
 
         def project_right(z_mx_b, z_mx_c):
-            early = keep.tile([P, 2, PIECE], F32, name="res_early")
+            early = keep.tile([P, 2, PIECE], F32, name="res_early", align_bytes=BURST)
             nc.scalar.copy(early[:], product(z_mx_b, 2, 2, PIECE)[:])
             nc.sync.dma_start(out_rows[:, 2:4, HALF : HALF + PIECE], early[:])
-            res = keep.tile([P, 4, HALF], F32, name="res_right")
+            res = keep.tile([P, 4, HALF], F32, name="res_right", align_bytes=BURST)
             nc.scalar.copy(res[:, 0:2, 0:PIECE], product(z_mx_b, 0, 2, PIECE)[:])
             for a in range(4):
                 acc = product(z_mx_c, a, 1, PIECE)

@@ -26,53 +26,41 @@ def tile_picked_scoremix_relu_p_kernel(tc, x_words, x_scales, d_words, d_scales,
     nc = tc.nc
     with ExitStack() as ctx:
         keep = ctx.enter_context(tc.tile_pool(name="keep", bufs=1))
+        turns = ctx.enter_context(tc.tile_pool(name="turns", bufs=1))
         psum = ctx.enter_context(tc.psum_pool(name="psum", bufs=8))
 
         kidx_sb = keep.tile([P, H // 16], U16, name="kidx_sb")
         offs_sb = keep.tile([P, S // 16], U16, name="offs_sb")
         nb_sb = keep.tile([P, S // 16], U16, name="nb_sb")
         gn_sb = keep.tile([P, PACK], F32, name="gn_sb")
-        nc.sync.dma_start(gn_sb[:], gn.rearrange("(p t) o -> p (t o)", t=PACK))
-        nc.sync.dma_start(kidx_sb[:], kidx)
-        w_rows = w1.rearrange("(p t) m -> p t m", t=PACK)
-        w_early = keep.tile([P, 2, N], F32, name="w_early", align_bytes=BURST)
-        nc.scalar.dma_start(w_early[:], w_rows[:, 0:2, :])
-        nc.sync.dma_start(offs_sb[:], offs)
-
         ds_win = keep.tile([P, G], U8, name="ds_win", align_bytes=BURST)
         xs_win = keep.tile([P, T], U8, name="xs_win", tag="window_turn", align_bytes=BURST)
         nc.vector.memset(ds_win[:].bitcast(I32), 0)
         nc.vector.memset(xs_win[:].bitcast(I32), 0)
+        nc.sync.dma_start(gn_sb[:], gn.rearrange("(p t) o -> p (t o)", t=PACK))
+        nc.sync.dma_start(kidx_sb[:], kidx)
+        nc.sync.dma_start(offs_sb[:], offs)
+        nc.sync.dma_start(nb_sb[:], nb)
         nc.sync.dma_start(ds_win[0:P:8, :].bitcast(I32), d_scales[0].bitcast(I32))
-        w_late = keep.tile([P, 2, N], F32, name="w_late", align_bytes=BURST)
-        nc.sync.dma_start(w_late[:], w_rows[:, 2:PACK, :])
         nc.sync.dma_start(xs_win[0:P:8, :].bitcast(I32), x_scales[0].bitcast(I32))
-
         dw_win = keep.tile([P, G], I32, name="dw_win", align_bytes=BURST)
         nc.sync.dma_start(dw_win[:], d_words[0].rearrange("p n t -> p (n t)").bitcast(I32))
-        xw_win = keep.tile([P, T], I32, name="xw_win", tag="x_turn", align_bytes=BURST)
+        xw_win = keep.tile([P, T], I32, name="xw_win", align_bytes=BURST)
         nc.sync.dma_start(xw_win[:], x_words[0].rearrange("p n t -> p (n t)").bitcast(I32))
-        nc.sync.dma_start(nb_sb[:], nb)
+        w_rows = w1.rearrange("(p t) m -> p t m", t=PACK)
+        w_first = keep.tile([P, PACK, P], F32, name="w_first", align_bytes=BURST)
+        nc.sync.dma_start(w_first[:], w_rows[:, :, 0:P])
 
         gn_sign = keep.tile([P, PACK], F32, name="gn_sign")
-        gn_half = keep.tile([P, PACK], F32, name="gn_half")
         gn_whole = keep.tile([P, PACK], F32, name="gn_whole")
-        nc.scalar.activation(gn_sign[:], gn_sb[:], ACT.Sign)
+        gn_half = keep.tile([P, PACK], F32, name="gn_half")
         nc.scalar.activation(gn_half[:], gn_sb[:], ACT.Abs, scale=0.0625 * 0.5)
         nc.scalar.activation(gn_whole[:], gn_sb[:], ACT.Abs, scale=0.0625)
+        nc.scalar.activation(gn_sign[:], gn_sb[:], ACT.Sign)
 
-        w_grouped = keep.tile([P, N, PACK], BF16, name="w_grouped", align_bytes=64)
-        w_pairs = keep.tile([P, 2, N, 2], BF16, name="w_pairs")
-
-        def sign_rows(u, raw):
-            for e in range(2):
-                t = 2 * u + e
-                nc.scalar.activation(w_pairs[:, u, :, e], raw[:, e, :], ACT.Copy, scale=gn_sign[:, t : t + 1])
-
-        sign_rows(0, w_early)
         ds_got = keep.tile([P, H], U8, name="ds_got")
         nc.vector.tensor_copy(ds_got[:], ds_win[:].indirect(kidx_sb[:]))
-        xs_got = keep.tile([P, S], U8, name="xs_got")
+        xs_got = turns.tile([P, S], U8, name="xs_got", offset=3840, align_bytes=BURST)
         nc.vector.tensor_copy(xs_got[:], xs_win[:].indirect(offs_sb[:]))
         moved = keep.tile([P, H + S], U8, name="moved", tag="window_turn", align_bytes=BURST)
         nc.vector.tensor_copy(
@@ -81,58 +69,100 @@ def tile_picked_scoremix_relu_p_kernel(tc, x_words, x_scales, d_words, d_scales,
         )
         nc.vector.tensor_copy(moved[:, H : H + S].bitcast(I32), xs_got[:].bitcast(I32))
         for r in range(1, PACK):
-            nc.scalar.dma_start(moved[r:P:32, :].bitcast(I32), moved[8 * r : P : 32, :].bitcast(I32))
-        sign_rows(1, w_late)
-        pair_words = w_pairs[:].rearrange("p u m e -> p u (m e)").bitcast(U32)
-        grouped_words = w_grouped[:].rearrange("p m t -> p (m t)").bitcast(U32).rearrange("p (m u) -> p m u", u=2)
-        nc.scalar.copy(
-            grouped_words.rearrange("p (c i) u -> p c u i", i=4), pair_words.rearrange("p u (c i) -> p c u i", i=4)
-        )
+            nc.sync.dma_start(moved[r:P:32, :].bitcast(I32), moved[8 * r : P : 32, :].bitcast(I32))
+        w_second = turns.tile([P, PACK, P], F32, name="w_second", offset=4096, align_bytes=BURST)
+        nc.sync.dma_start(w_second[:], w_rows[:, :, P:HALF])
+        w_right = turns.tile([P, PACK, HALF], F32, name="w_right", offset=0, align_bytes=BURST)
+        nc.sync.dma_start(w_right[:], w_rows[:, :, HALF:N])
 
         dw_got = keep.tile([P, H], U32, name="dw_got")
-        nc.vector.tensor_copy(dw_got[:], dw_win[:].bitcast(U32).indirect(kidx_sb[:]))
         d_codes = keep.tile([P, PACK, P], U32, name="d_codes", align_bytes=64)
-        nc.vector.tensor_copy(
-            d_codes[:].rearrange("p t (c i) -> p c t i", i=4), dw_got[:].rearrange("p (c i t) -> p c t i", t=PACK, i=4)
-        )
+        for h in range(2):
+            keys = slice(h * HALF, (h + 1) * HALF)
+            nc.vector.tensor_copy(dw_got[:, keys], dw_win[:].bitcast(U32).indirect(kidx_sb[:, 16 * h : 16 * (h + 1)]))
+        for h in range(2):
+            nc.vector.tensor_copy(
+                d_codes[:, :, 64 * h : 64 * (h + 1)].rearrange("p t (c i) -> p c t i", i=4),
+                dw_got[:, h * HALF : (h + 1) * HALF].rearrange("p (c i t) -> p c t i", t=PACK, i=4),
+            )
 
         x_codes = keep.tile([P, S], U32, name="x_codes", align_bytes=64)
-        for j0, n in ((0, PIECE), (PIECE, PIECE), (HALF, HALF)):
+        for h in range(2):
             nc.vector.tensor_copy(
-                x_codes[:, j0 : j0 + n], xw_win[:].bitcast(U32).indirect(offs_sb[:, j0 // 16 : (j0 + n) // 16])
+                x_codes[:, h * HALF : (h + 1) * HALF], xw_win[:].bitcast(U32).indirect(offs_sb[:, 16 * h : 16 * (h + 1)])
             )
 
         out_rows = out.rearrange("(a p) j -> p a j", p=P)
-        w_codes = keep.tile([P, N], U32, name="w_codes", tag="x_turn", align_bytes=BURST)
+        w_codes = keep.tile([P, N], U32, name="w_codes", align_bytes=64)
         w_scales = keep.tile([P, N], U8, name="w_scales", align_bytes=64)
-        nc.vector.quantize_mx(
-            out=w_codes[:].bitcast(FP8X4), scales=w_scales[:], in_=w_grouped[:].rearrange("p m t -> p (m t)")
+
+        signs = gn_sign[:].rearrange("p (o t) -> p o t", o=1).to_broadcast([P, P, PACK])
+
+        def quantise_w(h, grouped):
+            nc.vector.quantize_mx(
+                out=w_codes[:, h * HALF : (h + 1) * HALF].bitcast(FP8X4),
+                scales=w_scales[:, h * HALF : (h + 1) * HALF],
+                in_=grouped[:].rearrange("p m t -> p (m t)"),
+            )
+
+        grouped_left = keep.tile([P, HALF, PACK], BF16, name="grouped_left", tag="grouped_turn", align_bytes=64)
+        w_pairs = keep.tile([P, 2, P, 2], BF16, name="w_pairs")
+        for t in range(PACK):
+            nc.scalar.activation(w_pairs[:, t // 2, :, t % 2], w_first[:, t, :], ACT.Copy, scale=gn_sign[:, t : t + 1])
+        pair_words = w_pairs[:].rearrange("p u m e -> p u (m e)").bitcast(U32)
+        grouped_words = grouped_left[:, 0:P, :].rearrange("p m t -> p (m t)").bitcast(U32).rearrange("p (m u) -> p m u", u=2)
+        nc.scalar.copy(
+            grouped_words.rearrange("p (c i) u -> p c u i", i=4), pair_words.rearrange("p u (c i) -> p c u i", i=4)
         )
+        nc.vector.tensor_tensor(
+            grouped_left[:, P:HALF, :].rearrange("p (c i) t -> p c t i", i=2),
+            w_second[:].rearrange("p t (c i) -> p c t i", i=2),
+            gn_sign[:].rearrange("p (o t i) -> p o t i", o=1, i=1).to_broadcast([P, P // 2, PACK, 2]),
+            ALU.mult,
+        )
+        quantise_w(0, grouped_left)
+        grouped_right = keep.tile([P, HALF, PACK], BF16, name="grouped_right", tag="grouped_turn", align_bytes=64)
+        for a in range(2):
+            cols = slice(a * P, (a + 1) * P)
+            nc.gpsimd.tensor_tensor(
+                grouped_right[:, cols, :], w_right[:, :, cols].rearrange("p t m -> p m t"), signs, ALU.mult
+            )
 
-        def mix(mixed, t, whole, j0, n):
-            nc.vector.tensor_tensor(mixed, halved[t][:].indirect(nb_sb[:, j0 // 16 : (j0 + n) // 16]), whole, ALU.add)
+        halved = [keep.tile([P, S], F32, name="halved%d" % t) for t in range(PACK)]
 
-        def rectify(mixed, n, engine, tag):
-            z = keep.tile([P, n, PACK], BF16, name="z_" + tag, align_bytes=64)
-            dst = z[:].rearrange("p (c i) t -> p c t i", i=2)
-            src = mixed.rearrange("p t (c i) -> p c t i", i=2)
+        def score(t, j0, n, engine):
+            acc = psum.tile([P, n], F32, name="acc", tag="bank")
+            nc.tensor.matmul_mx(
+                out=acc[:],
+                lhsT=d_codes[:, t, :].bitcast(FP8X4),
+                lhsT_scale=moved[:, t * P : (t + 1) * P],
+                rhs=x_codes[:, j0 : j0 + n].bitcast(FP8X4),
+                rhs_scale=moved[:, H + j0 : H + j0 + n],
+                start=True,
+                stop=True,
+            )
             if engine is nc.scalar:
-                nc.scalar.activation(dst, src, ACT.Relu)
+                nc.scalar.activation(halved[t][:, j0 : j0 + n], acc[:], ACT.Copy, scale=gn_half[:, t : t + 1])
             else:
-                nc.vector.tensor_scalar(dst, src, 0.0, None, ALU.max)
-            return z
+                nc.vector.tensor_scalar(halved[t][:, j0 : j0 + n], acc[:], gn_half[:, t : t + 1], None, ALU.mult)
+            return acc
 
-        def quantise(z, j0, n):
-            z_codes = keep.tile([P, n], U32, name="z_codes%d" % j0, align_bytes=64)
-            z_scales = keep.tile([P, n], U8, name="z_scales%d" % j0, align_bytes=64)
+        def rectify(z, mixed):
+            nc.vector.tensor_scalar(
+                z[:].rearrange("p (c i) t -> p c t i", i=2), mixed.rearrange("p t (c i) -> p c t i", i=2), 0.0, None, ALU.max
+            )
+
+        def quantise(z, q):
+            z_codes = keep.tile([P, PIECE], U32, name="z_codes%d" % q, align_bytes=64)
+            z_scales = keep.tile([P, PIECE], U8, name="z_scales%d" % q, align_bytes=64)
             nc.vector.quantize_mx(
                 out=z_codes[:].bitcast(FP8X4), scales=z_scales[:], in_=z[:].rearrange("p j t -> p (j t)")
             )
             return z_codes, z_scales
 
-        def product(z_mx, first, blocks, n):
+        def product(z_mx, first, blocks):
             z_codes, z_scales = z_mx
-            acc = psum.tile([P, blocks, n], F32, name="acc2", tag="bank")
+            acc = psum.tile([P, blocks, PIECE], F32, name="acc2", tag="bank")
             for a in range(blocks):
                 m_cols = slice((first + a) * P, (first + a + 1) * P)
                 nc.tensor.matmul_mx(
@@ -146,80 +176,80 @@ def tile_picked_scoremix_relu_p_kernel(tc, x_words, x_scales, d_words, d_scales,
                 )
             return acc
 
-        def project(z_mx, j0):
-            for first in (0, 2):
-                res = keep.tile([P, 2, PIECE], F32, name="res%d_%d" % (j0, first), align_bytes=BURST)
-                nc.scalar.copy(res[:], product(z_mx, first, 2, PIECE)[:])
-                nc.sync.dma_start(out_rows[:, first : first + 2, j0 : j0 + PIECE], res[:])
-
-        def project_right(z_mx_b, z_mx_c):
-            early = keep.tile([P, 2, PIECE], F32, name="res_early", align_bytes=BURST)
-            nc.scalar.copy(early[:], product(z_mx_b, 2, 2, PIECE)[:])
-            nc.sync.dma_start(out_rows[:, 2:4, HALF : HALF + PIECE], early[:])
-            res = keep.tile([P, 4, HALF], F32, name="res_right", align_bytes=BURST)
-            nc.scalar.copy(res[:, 0:2, 0:PIECE], product(z_mx_b, 0, 2, PIECE)[:])
-            for a in range(4):
-                acc = product(z_mx_c, a, 1, PIECE)
-                if a % 2 == 1:
-                    nc.scalar.copy(res[:, a : a + 1, PIECE:HALF], acc[:])
+        def project(z_mx, q, engines):
+            for first, engine in zip((0, 2), engines):
+                res = keep.tile([P, 2, PIECE], F32, name="res%d_%d" % (q, first), align_bytes=BURST)
+                acc = product(z_mx, first, 2)
+                if engine is nc.scalar:
+                    nc.scalar.copy(res[:], acc[:])
                 else:
-                    nc.vector.tensor_copy(res[:, a : a + 1, PIECE:HALF], acc[:])
-                if a < 2:
-                    nc.sync.dma_start(out_rows[:, a : a + 1, HALF:S], res[:, a : a + 1, :])
-            nc.scalar.dma_start(out_rows[:, 2:4, HALF + PIECE : S], res[:, 2:4, PIECE:HALF])
+                    nc.vector.tensor_copy(res[:], acc[:])
+                nc.sync.dma_start(out_rows[:, first : first + 2, q * PIECE : (q + 1) * PIECE], res[:])
 
-        halved = [keep.tile([P, S], F32, name="halved%d" % t) for t in range(PACK)]
-        left = [keep.tile([P, HALF], F32, name="left%d" % t) for t in range(PACK)]
-        mixed_a = keep.tile([P, PACK, HALF], F32, name="mixed_a")
+        def fetch(dst, t, j0, n, engine):
+            window = halved[t][:].indirect(nb_sb[:, j0 // 16 : (j0 + n) // 16])
+            if engine is nc.scalar:
+                nc.scalar.activation(dst, window, ACT.Copy)
+            else:
+                nc.vector.tensor_copy(dst, window)
 
-        def score(t, j0, n):
-            acc = psum.tile([P, n], F32, name="acc", tag="bank")
-            nc.tensor.matmul_mx(
-                out=acc[:],
-                lhsT=d_codes[:, t, :].bitcast(FP8X4),
-                lhsT_scale=moved[:, t * P : (t + 1) * P],
-                rhs=x_codes[:, j0 : j0 + n].bitcast(FP8X4),
-                rhs_scale=moved[:, H + j0 : H + j0 + n],
-                start=True,
-                stop=True,
+        mixed_left = keep.tile([P, PACK, HALF], F32, name="mixed_left")
+        fetched_left = [keep.tile([P, HALF], F32, name="fetched_left%d" % t, tag="fetch_turn%d" % t) for t in range(PACK)]
+
+        def add_left(t):
+            nc.vector.scalar_tensor_tensor(
+                mixed_left[:, t, :], banks[t][:, 0:HALF], gn_whole[:, t : t + 1], fetched_left[t][:], ALU.mult, ALU.add
             )
-            nc.scalar.activation(halved[t][:, j0 : j0 + n], acc[:], ACT.Copy, scale=gn_half[:, t : t + 1])
-            return acc
 
-        last = PACK - 1
-        for t in range(2):
-            score(t, 0, PIECE)
-        for t in range(2):
-            score(t, PIECE, PIECE)
-            nc.vector.tensor_scalar(left[t][:], halved[t][:, 0:HALF], 2.0, None, ALU.mult)
-        score(2, 0, HALF)
-        nc.vector.tensor_scalar(left[2][:], halved[2][:, 0:HALF], 2.0, None, ALU.mult)
-        for t in range(last):
-            score(t, HALF, HALF)
-            mix(mixed_a[:, t, :], t, left[t][:], 0, HALF)
-        bank = score(last, 0, S)
-        nc.scalar.activation(left[last][:], bank[:, 0:HALF], ACT.Copy, scale=gn_whole[:, last : last + 1])
-        mix(mixed_a[:, last, :], last, left[last][:], 0, HALF)
+        banks = [score(t, 0, HALF, nc.scalar) for t in range(2)]
+        score(0, HALF, HALF, nc.scalar)
+        score(1, HALF, HALF, nc.vector)
+        fetch(fetched_left[0][:], 0, 0, HALF, nc.scalar)
+        fetch(fetched_left[1][:], 1, 0, HALF, nc.vector)
+        banks.append(score(2, 0, S, nc.scalar))
+        add_left(0)
+        banks.append(score(3, 0, S, nc.vector))
+        fetch(fetched_left[2][:], 2, 0, HALF, nc.scalar)
+        add_left(1)
+        fetch(fetched_left[3][:], 3, 0, HALF, nc.scalar)
+        add_left(2)
+        add_left(3)
 
-        right = []
+        z_0 = turns.tile([P, PIECE, PACK], BF16, name="z_0", offset=0, align_bytes=BURST)
+        mixed_2 = turns.tile([P, PACK, PIECE], F32, name="mixed_2", offset=1024, align_bytes=BURST)
+        mixed_3 = turns.tile([P, PACK, PIECE], F32, name="mixed_3", offset=3072, align_bytes=BURST)
+        fetched_2 = keep.tile([P, PACK, PIECE], F32, name="fetched_2", tag="fetch_turn0")
+        fetched_3a = keep.tile([P, 2, PIECE], F32, name="fetched_3a", tag="fetch_turn3")
+        fetched_3b = turns.tile([P, 2, PIECE], F32, name="fetched_3b", offset=0, align_bytes=BURST)
+        fetched = {(2, t): fetched_2[:, t, :] for t in range(PACK)}
         for t in range(PACK):
-            doubled = keep.tile([P, HALF], F32, name="right%d" % t)
-            nc.scalar.activation(doubled[:], halved[t][:, HALF:S], ACT.Copy, scale=2.0)
-            right.append(doubled)
+            fetched[3, t] = (fetched_3a, fetched_3b)[t // 2][:, t % 2, :]
 
-        mixed_b = keep.tile([P, PACK, PIECE], F32, name="mixed_b")
-        mixed_c = mixed_a[:, 0:2, :].rearrange("p a (b j) -> p (a b) j", j=PIECE)
-        z_0 = rectify(mixed_a[:, :, 0:PIECE], PIECE, nc.scalar, "0")
-        z_1 = rectify(mixed_a[:, :, PIECE:HALF], PIECE, nc.scalar, "1")
+        def add(mixed, q, t):
+            nc.vector.scalar_tensor_tensor(
+                mixed[:, t, :], halved[t][:, q * PIECE : (q + 1) * PIECE], 2.0, fetched[q, t], ALU.mult, ALU.add
+            )
+
         for t in range(PACK):
-            mix(mixed_b[:, t, :], t, right[t][:, 0:PIECE], HALF, PIECE)
-        z_2 = rectify(mixed_b[:], PIECE, nc.scalar, "2")
-        project(quantise(z_0, 0, PIECE), 0)
-        for t in (0, 2):
-            mix(mixed_c[:, t, :], t, right[t][:, PIECE:HALF], HALF + PIECE, PIECE)
-        project(quantise(z_1, PIECE, PIECE), PIECE)
-        for t in (1, 3):
-            mix(mixed_c[:, t, :], t, right[t][:, PIECE:HALF], HALF + PIECE, PIECE)
-        z_2_mx = quantise(z_2, HALF, PIECE)
-        z_3 = rectify(mixed_c, PIECE, nc.vector, "3")
-        project_right(z_2_mx, quantise(z_3, HALF + PIECE, PIECE))
+            fetch(fetched[2, t], t, 2 * PIECE, PIECE, nc.scalar)
+        for t in range(2):
+            fetch(fetched[3, t], t, 3 * PIECE, PIECE, nc.scalar)
+        quantise_w(1, grouped_right)
+        rectify(z_0, mixed_left[:, :, 0:PIECE])
+        project(quantise(z_0, 0), 0, (nc.scalar, nc.scalar))
+        for t in range(2, PACK):
+            fetch(fetched[3, t], t, 3 * PIECE, PIECE, nc.scalar)
+        add(mixed_2, 2, 0)
+        z_1 = keep.tile([P, PIECE, PACK], BF16, name="z_1", tag="grouped_turn", align_bytes=64)
+        rectify(z_1, mixed_left[:, :, PIECE:HALF])
+        project(quantise(z_1, 1), 1, (nc.scalar, nc.scalar))
+        for t in range(1, PACK):
+            add(mixed_2, 2, t)
+        z_2 = keep.tile([P, PIECE, PACK], BF16, name="z_2", align_bytes=64)
+        rectify(z_2, mixed_2[:])
+        project(quantise(z_2, 2), 2, (nc.scalar, nc.scalar))
+        for t in range(PACK):
+            add(mixed_3, 3, t)
+        z_3 = keep.tile([P, PIECE, PACK], BF16, name="z_3", align_bytes=64)
+        rectify(z_3, mixed_3[:])
+        project(quantise(z_3, 3), 3, (nc.scalar, nc.vector))

from contextlib import ExitStack

import concourse.mybir as mybir

K, T, S, N, G, H = 512, 2048, 512, 512, 2048, 512
FLOPS = 2 * K * H * S + 2 * H * N * S

F32 = mybir.dt.float32
BF16 = mybir.dt.bfloat16
I32 = mybir.dt.int32
U32 = mybir.dt.uint32
U16 = mybir.dt.uint16
U8 = mybir.dt.uint8
FP8X4 = mybir.dt.float8_e4m3fn_x4
ACT = mybir.ActivationFunctionType
ALU = mybir.AluOpType

P = 128
PACK = 4
HALF = 256
PIECE = 128
BURST = 256


def tile_picked_scoremix_relu_p_kernel(tc, x_words, x_scales, d_words, d_scales, gn, w1, offs, kidx, nb, out):
    nc = tc.nc
    with ExitStack() as ctx:
        keep = ctx.enter_context(tc.tile_pool(name="keep", bufs=1))
        turns = ctx.enter_context(tc.tile_pool(name="turns", bufs=1))
        psum = ctx.enter_context(tc.psum_pool(name="psum", bufs=8))

        kidx_sb = keep.tile([P, H // 16], U16, name="kidx_sb")
        offs_sb = keep.tile([P, S // 16], U16, name="offs_sb")
        nb_sb = keep.tile([P, S // 16], U16, name="nb_sb")
        gn_sb = keep.tile([P, PACK], F32, name="gn_sb")
        ds_win = keep.tile([P, G], U8, name="ds_win", align_bytes=BURST)
        xs_win = keep.tile([P, T], U8, name="xs_win", tag="window_turn", align_bytes=BURST)
        nc.vector.memset(ds_win[:].bitcast(I32), 0)
        nc.vector.memset(xs_win[:].bitcast(I32), 0)
        nc.sync.dma_start(gn_sb[:], gn.rearrange("(p t) o -> p (t o)", t=PACK))
        nc.sync.dma_start(kidx_sb[:], kidx)
        nc.sync.dma_start(offs_sb[:], offs)
        nc.sync.dma_start(nb_sb[:], nb)
        nc.sync.dma_start(ds_win[0:P:8, :].bitcast(I32), d_scales[0].bitcast(I32))
        nc.sync.dma_start(xs_win[0:P:8, :].bitcast(I32), x_scales[0].bitcast(I32))
        dw_win = keep.tile([P, G], I32, name="dw_win", align_bytes=BURST)
        nc.sync.dma_start(dw_win[:], d_words[0].rearrange("p n t -> p (n t)").bitcast(I32))
        xw_win = keep.tile([P, T], I32, name="xw_win", align_bytes=BURST)
        nc.sync.dma_start(xw_win[:], x_words[0].rearrange("p n t -> p (n t)").bitcast(I32))
        w_rows = w1.rearrange("(p t) m -> p t m", t=PACK)
        w_first = keep.tile([P, PACK, P], F32, name="w_first", align_bytes=BURST)
        nc.sync.dma_start(w_first[:], w_rows[:, :, 0:P])

        gn_sign = keep.tile([P, PACK], F32, name="gn_sign")
        gn_whole = keep.tile([P, PACK], F32, name="gn_whole")
        gn_half = keep.tile([P, PACK], F32, name="gn_half")
        nc.scalar.activation(gn_half[:], gn_sb[:], ACT.Abs, scale=0.0625 * 0.5)
        nc.scalar.activation(gn_whole[:], gn_sb[:], ACT.Abs, scale=0.0625)
        nc.scalar.activation(gn_sign[:], gn_sb[:], ACT.Sign)

        ds_got = keep.tile([P, H], U8, name="ds_got")
        nc.vector.tensor_copy(ds_got[:], ds_win[:].indirect(kidx_sb[:]))
        xs_got = turns.tile([P, S], U8, name="xs_got", offset=3840, align_bytes=BURST)
        nc.vector.tensor_copy(xs_got[:], xs_win[:].indirect(offs_sb[:]))
        moved = keep.tile([P, H + S], U8, name="moved", tag="window_turn", align_bytes=BURST)
        nc.vector.tensor_copy(
            moved[:, 0:H].rearrange("p (t c i) -> p c t i", t=PACK, i=16),
            ds_got[:].rearrange("p (c i t) -> p c t i", t=PACK, i=16),
        )
        nc.vector.tensor_copy(moved[:, H : H + S].bitcast(I32), xs_got[:].bitcast(I32))
        for r in range(1, PACK):
            nc.sync.dma_start(moved[r:P:32, :].bitcast(I32), moved[8 * r : P : 32, :].bitcast(I32))
        w_second = turns.tile([P, PACK, P], F32, name="w_second", offset=4096, align_bytes=BURST)
        nc.sync.dma_start(w_second[:], w_rows[:, :, P:HALF])
        w_right = turns.tile([P, PACK, HALF], F32, name="w_right", offset=0, align_bytes=BURST)
        nc.sync.dma_start(w_right[:], w_rows[:, :, HALF:N])

        dw_got = keep.tile([P, H], U32, name="dw_got")
        d_codes = keep.tile([P, PACK, P], U32, name="d_codes", align_bytes=64)
        for h in range(2):
            keys = slice(h * HALF, (h + 1) * HALF)
            nc.vector.tensor_copy(dw_got[:, keys], dw_win[:].bitcast(U32).indirect(kidx_sb[:, 16 * h : 16 * (h + 1)]))
        for h in range(2):
            nc.vector.tensor_copy(
                d_codes[:, :, 64 * h : 64 * (h + 1)].rearrange("p t (c i) -> p c t i", i=4),
                dw_got[:, h * HALF : (h + 1) * HALF].rearrange("p (c i t) -> p c t i", t=PACK, i=4),
            )

        x_codes = keep.tile([P, S], U32, name="x_codes", align_bytes=64)
        for h in range(2):
            nc.vector.tensor_copy(
                x_codes[:, h * HALF : (h + 1) * HALF], xw_win[:].bitcast(U32).indirect(offs_sb[:, 16 * h : 16 * (h + 1)])
            )

        out_rows = out.rearrange("(a p) j -> p a j", p=P)
        w_codes = keep.tile([P, N], U32, name="w_codes", align_bytes=64)
        w_scales = keep.tile([P, N], U8, name="w_scales", align_bytes=64)

        signs = gn_sign[:].rearrange("p (o t) -> p o t", o=1).to_broadcast([P, P, PACK])

        def quantise_w(h, grouped):
            nc.vector.quantize_mx(
                out=w_codes[:, h * HALF : (h + 1) * HALF].bitcast(FP8X4),
                scales=w_scales[:, h * HALF : (h + 1) * HALF],
                in_=grouped[:].rearrange("p m t -> p (m t)"),
            )

        grouped_left = keep.tile([P, HALF, PACK], BF16, name="grouped_left", tag="grouped_turn", align_bytes=64)
        w_pairs = keep.tile([P, 2, P, 2], BF16, name="w_pairs")
        for t in range(PACK):
            nc.scalar.activation(w_pairs[:, t // 2, :, t % 2], w_first[:, t, :], ACT.Copy, scale=gn_sign[:, t : t + 1])
        pair_words = w_pairs[:].rearrange("p u m e -> p u (m e)").bitcast(U32)
        grouped_words = grouped_left[:, 0:P, :].rearrange("p m t -> p (m t)").bitcast(U32).rearrange("p (m u) -> p m u", u=2)
        nc.scalar.copy(
            grouped_words.rearrange("p (c i) u -> p c u i", i=4), pair_words.rearrange("p u (c i) -> p c u i", i=4)
        )
        nc.vector.tensor_tensor(
            grouped_left[:, P:HALF, :].rearrange("p (c i) t -> p c t i", i=2),
            w_second[:].rearrange("p t (c i) -> p c t i", i=2),
            gn_sign[:].rearrange("p (o t i) -> p o t i", o=1, i=1).to_broadcast([P, P // 2, PACK, 2]),
            ALU.mult,
        )
        quantise_w(0, grouped_left)
        grouped_right = keep.tile([P, HALF, PACK], BF16, name="grouped_right", tag="grouped_turn", align_bytes=64)
        for a in range(2):
            cols = slice(a * P, (a + 1) * P)
            nc.gpsimd.tensor_tensor(
                grouped_right[:, cols, :], w_right[:, :, cols].rearrange("p t m -> p m t"), signs, ALU.mult
            )

        halved = [keep.tile([P, S], F32, name="halved%d" % t) for t in range(PACK)]

        def score(t, j0, n, engine):
            acc = psum.tile([P, n], F32, name="acc", tag="bank")
            nc.tensor.matmul_mx(
                out=acc[:],
                lhsT=d_codes[:, t, :].bitcast(FP8X4),
                lhsT_scale=moved[:, t * P : (t + 1) * P],
                rhs=x_codes[:, j0 : j0 + n].bitcast(FP8X4),
                rhs_scale=moved[:, H + j0 : H + j0 + n],
                start=True,
                stop=True,
            )
            if engine is nc.scalar:
                nc.scalar.activation(halved[t][:, j0 : j0 + n], acc[:], ACT.Copy, scale=gn_half[:, t : t + 1])
            else:
                nc.vector.tensor_scalar(halved[t][:, j0 : j0 + n], acc[:], gn_half[:, t : t + 1], None, ALU.mult)
            return acc

        def rectify(z, mixed):
            nc.vector.tensor_scalar(
                z[:].rearrange("p (c i) t -> p c t i", i=2), mixed.rearrange("p t (c i) -> p c t i", i=2), 0.0, None, ALU.max
            )

        def quantise(z, q):
            z_codes = keep.tile([P, PIECE], U32, name="z_codes%d" % q, align_bytes=64)
            z_scales = keep.tile([P, PIECE], U8, name="z_scales%d" % q, align_bytes=64)
            nc.vector.quantize_mx(
                out=z_codes[:].bitcast(FP8X4), scales=z_scales[:], in_=z[:].rearrange("p j t -> p (j t)")
            )
            return z_codes, z_scales

        def product(z_mx, first, blocks):
            z_codes, z_scales = z_mx
            acc = psum.tile([P, blocks, PIECE], F32, name="acc2", tag="bank")
            for a in range(blocks):
                m_cols = slice((first + a) * P, (first + a + 1) * P)
                nc.tensor.matmul_mx(
                    out=acc[:, a, :],
                    lhsT=w_codes[:, m_cols].bitcast(FP8X4),
                    lhsT_scale=w_scales[:, m_cols],
                    rhs=z_codes[:].bitcast(FP8X4),
                    rhs_scale=z_scales[:],
                    start=True,
                    stop=True,
                )
            return acc

        def project(z_mx, q, engines):
            for first, engine in zip((0, 2), engines):
                res = keep.tile([P, 2, PIECE], F32, name="res%d_%d" % (q, first), align_bytes=BURST)
                acc = product(z_mx, first, 2)
                if engine is nc.scalar:
                    nc.scalar.copy(res[:], acc[:])
                else:
                    nc.vector.tensor_copy(res[:], acc[:])
                nc.sync.dma_start(out_rows[:, first : first + 2, q * PIECE : (q + 1) * PIECE], res[:])

        def fetch(dst, t, j0, n, engine):
            window = halved[t][:].indirect(nb_sb[:, j0 // 16 : (j0 + n) // 16])
            if engine is nc.scalar:
                nc.scalar.activation(dst, window, ACT.Copy)
            else:
                nc.vector.tensor_copy(dst, window)

        mixed_left = keep.tile([P, PACK, HALF], F32, name="mixed_left")
        fetched_left = [keep.tile([P, HALF], F32, name="fetched_left%d" % t, tag="fetch_turn%d" % t) for t in range(PACK)]

        def add_left(t):
            nc.vector.scalar_tensor_tensor(
                mixed_left[:, t, :], banks[t][:, 0:HALF], gn_whole[:, t : t + 1], fetched_left[t][:], ALU.mult, ALU.add
            )

        banks = [score(t, 0, HALF, nc.scalar) for t in range(2)]
        score(0, HALF, HALF, nc.scalar)
        score(1, HALF, HALF, nc.vector)
        fetch(fetched_left[0][:], 0, 0, HALF, nc.scalar)
        fetch(fetched_left[1][:], 1, 0, HALF, nc.vector)
        banks.append(score(2, 0, S, nc.scalar))
        add_left(0)
        banks.append(score(3, 0, S, nc.vector))
        fetch(fetched_left[2][:], 2, 0, HALF, nc.scalar)
        add_left(1)
        fetch(fetched_left[3][:], 3, 0, HALF, nc.scalar)
        add_left(2)
        add_left(3)

        z_0 = turns.tile([P, PIECE, PACK], BF16, name="z_0", offset=0, align_bytes=BURST)
        mixed_2 = turns.tile([P, PACK, PIECE], F32, name="mixed_2", offset=1024, align_bytes=BURST)
        mixed_3 = turns.tile([P, PACK, PIECE], F32, name="mixed_3", offset=3072, align_bytes=BURST)
        fetched_2 = keep.tile([P, PACK, PIECE], F32, name="fetched_2", tag="fetch_turn0")
        fetched_3a = keep.tile([P, 2, PIECE], F32, name="fetched_3a", tag="fetch_turn3")
        fetched_3b = turns.tile([P, 2, PIECE], F32, name="fetched_3b", offset=0, align_bytes=BURST)
        fetched = {(2, t): fetched_2[:, t, :] for t in range(PACK)}
        for t in range(PACK):
            fetched[3, t] = (fetched_3a, fetched_3b)[t // 2][:, t % 2, :]

        def add(mixed, q, t):
            nc.vector.scalar_tensor_tensor(
                mixed[:, t, :], halved[t][:, q * PIECE : (q + 1) * PIECE], 2.0, fetched[q, t], ALU.mult, ALU.add
            )

        for t in range(PACK):
            fetch(fetched[2, t], t, 2 * PIECE, PIECE, nc.scalar)
        for t in range(2):
            fetch(fetched[3, t], t, 3 * PIECE, PIECE, nc.scalar)
        quantise_w(1, grouped_right)
        rectify(z_0, mixed_left[:, :, 0:PIECE])
        project(quantise(z_0, 0), 0, (nc.scalar, nc.scalar))
        for t in range(2, PACK):
            fetch(fetched[3, t], t, 3 * PIECE, PIECE, nc.scalar)
        add(mixed_2, 2, 0)
        z_1 = keep.tile([P, PIECE, PACK], BF16, name="z_1", tag="grouped_turn", align_bytes=64)
        rectify(z_1, mixed_left[:, :, PIECE:HALF])
        project(quantise(z_1, 1), 1, (nc.scalar, nc.scalar))
        for t in range(1, PACK):
            add(mixed_2, 2, t)
        z_2 = keep.tile([P, PIECE, PACK], BF16, name="z_2", align_bytes=64)
        rectify(z_2, mixed_2[:])
        project(quantise(z_2, 2), 2, (nc.scalar, nc.scalar))
        for t in range(PACK):
            add(mixed_3, 3, t)
        z_3 = keep.tile([P, PIECE, PACK], BF16, name="z_3", align_bytes=64)
        rectify(z_3, mixed_3[:])
        project(quantise(z_3, 3), 3, (nc.scalar, nc.vector))
